import numpy as np
import ml_dtypes


def mxq(x, axis, fmt="e4m3"):
    dtype, down = {"e4m3": (ml_dtypes.float8_e4m3fn, 7), "e5m2": (ml_dtypes.float8_e5m2, 14)}[fmt]
    v = np.moveaxis(np.asarray(x, np.float32).astype(ml_dtypes.bfloat16).astype(np.float64), axis, -1)
    blocks = v.reshape(v.shape[:-1] + (-1, 32))
    amax = np.abs(blocks).max(-1, keepdims=True)
    byte = np.maximum(np.where(amax > 0, np.frexp(amax)[1] - 1 + 127, 0) - down, 1)
    scale = np.exp2(byte - 127.0)
    codes = (blocks / scale).astype(np.float32).astype(dtype).astype(np.float64)
    return np.moveaxis((codes * scale).reshape(v.shape), -1, axis)


WIDE = False


def mx_kscale(k):
    if not WIDE:
        return np.ones(k)
    levels = np.array([10, -10, 5, -5, 0])
    if k % 512:
        return np.exp2(np.random.permutation(np.resize(levels, k // 32))).repeat(32)
    a = np.empty((k // 512, 16))
    for p in range(k // 512):
        a[p, :8] = np.random.permutation(np.resize(levels, 8))
        for g in range(8):
            far = levels[np.abs(levels - a[p, g]) >= 10]
            a[p, g + 8] = far[np.random.randint(len(far))]
    return np.exp2(a.ravel()).repeat(32)


def f64(x):
    return np.asarray(x).astype(np.float64)


def striped8(idx):
    return np.concatenate([v.reshape(-1, 16).T for v in idx]).astype(np.uint16)


def unstriped8(offs):
    return np.stack([offs[16 * g:16 * g + 16].T.reshape(-1) for g in range(8)]).astype(np.int64)


E2M1 = np.array([0.0, 0.5, 1.0, 1.5, 2.0, 3.0, 4.0, 6.0, -0.0, -0.5, -1.0, -1.5, -2.0, -3.0, -4.0, -6.0])


def pack_weight(w, fmt):
    k, n = w.shape
    w = f64(np.asarray(w, np.float32).astype(ml_dtypes.bfloat16)).reshape(k // 32, 32, n)
    amax = np.abs(w).max(1)
    if fmt == "e4m3":
        byte = np.frexp(amax)[1] - 1 + 127 - 7
    else:
        mant, ex = np.frexp(amax / 6.0)
        byte = np.where(mant > 0.5, ex, ex - 1) + 127
    byte = np.clip(np.where(amax > 0, byte, 1), 1, 254)
    scaled = (w * np.exp2(127.0 - byte)[:, None, :]).reshape(k, n).astype(np.float32)
    by_word = np.ascontiguousarray(scaled.reshape(k // 512, 128, 4, n).transpose(0, 1, 3, 2))
    if fmt == "e4m3":
        words = by_word.astype(ml_dtypes.float8_e4m3fn).view(np.uint8)
    else:
        c = by_word.astype(ml_dtypes.float4_e2m1fn).view(np.uint8) & 0xF
        words = (c[..., 0::2] | (c[..., 1::2] << 4)).reshape(k // 512, 128, 2 * n)
    return np.ascontiguousarray(words), np.ascontiguousarray(byte.astype(np.uint8).reshape(k // 512, 16, n))


def unpack_weight(words, scales, fmt):
    g, _, n = scales.shape
    words = np.ascontiguousarray(words).reshape(g, 128, n, -1)
    if fmt == "e4m3":
        vals = words.view(ml_dtypes.float8_e4m3fn).astype(np.float64)
    else:
        nib = np.empty((g, 128, n, 4), np.uint8)
        nib[..., 0::2] = words & 0xF
        nib[..., 1::2] = words >> 4
        vals = E2M1[nib]
    vals = vals * np.repeat(np.exp2(scales.astype(np.float64) - 127.0), 8, axis=1)[..., None]
    return vals.transpose(0, 1, 3, 2).reshape(g * 512, n)


K, L, M, T, S = 512, 512, 1024, 2048, 512


def setup_inputs():
    n = np.random.standard_normal
    s1 = mx_kscale(K)[:, None]
    s2 = mx_kscale(L)[:, None]
    p_w4 = pack_weight(n((K, M)) / np.sqrt(K) / s1, "e2m1")
    return {
        "xT": (n((K, T)) * s1).astype(np.float32),
        "w4_words": p_w4[0],
        "w4_scales": p_w4[1],
        "c": (n((L, S)) * s2).astype(np.float32),
        "u": (n((L, M)) / np.sqrt(L) / s2).astype(np.float32),
        "wgt": np.repeat(np.random.uniform(0.5, 2.0, (8, S)), 16, axis=0).astype(np.float32),
        "b": (0.3 * n(1024)).astype(np.float32),
        "offs": striped8(np.stack([np.random.permutation(T)[:S] for _ in range(8)])),
    }


def reference(xT, w4_words, w4_scales, c, u, wgt, b, offs):
    idx = unstriped8(offs)
    group = np.arange(K) % 512 // 64
    xg = f64(wgt)[np.arange(K) // 4 % 128] * f64(xT)[np.arange(K)[:, None], idx[group]]
    xT_ = mxq(xg, 0, "e4m3")
    w4_ = unpack_weight(w4_words, w4_scales, "e2m1")
    c_ = mxq(f64(c), 0, "e4m3")
    u_ = mxq(f64(u), 0, "e4m3")
    y = w4_.T @ xT_ + u_.T @ c_
    return y + f64(b)[:, None]

@@ -1,0 +1,183 @@
+from contextlib import ExitStack
+
+import concourse.mybir as mybir
+from concourse.masks import make_identity
+
+F32 = mybir.dt.float32
+BF16 = mybir.dt.bfloat16
+I32 = mybir.dt.int32
+U32 = mybir.dt.uint32
+U16 = mybir.dt.uint16
+U8 = mybir.dt.uint8
+E4M3X4 = mybir.dt.float8_e4m3fn_x4
+E2M1X4 = mybir.dt.float4_e2m1fn_x4
+MULT = mybir.AluOpType.mult
+ADD = mybir.AluOpType.add
+IDENTITY = mybir.ActivationFunctionType.Identity
+
+P = 128
+PACK = 4
+K, L, M, T, S = 512, 512, 1024, 2048, 512
+NB = M // P
+HEADS = 8
+U_WIDTHS = (256, 256, 256, 128, 128,)
+U_STARTS = (0, 256, 512, 768, 896,)
+U_SCALAR = (0, 192, 64, 0, 64,)
+C_SCALAR = 256
+G_CUTS = (0, 320, 512)
+PAIR0_ON = "VV"
+PAIR1_ON = "VS"
+DRAIN_ON = "SSSVVVSV"
+
+FLOPS = 2 * M * S * (K + L)
+
+
+def tile_list_hmix_bias_kernel(tc, xT, w4_words, w4_scales, c, u, wgt, b, offs, out):
+    nc = tc.nc
+    with ExitStack() as ctx:
+        keep = ctx.enter_context(tc.tile_pool(name="keep", bufs=1))
+        psum = ctx.enter_context(tc.psum_pool(name="psum", bufs=1))
+
+        offsets = keep.tile([P, S // 16], U16, name="offsets")
+        weights = keep.tile([P, S], F32, name="weights")
+        planes = [keep.tile([P, T], F32, name=f"plane{i}") for i in range(PACK)]
+        c_raw = keep.tile([P, PACK, S], F32, name="c_raw")
+        u_raw = [keep.tile([P, PACK, w], F32, name=f"u_raw{q}") for q, w in enumerate(U_WIDTHS)]
+        w4_t = [keep.tile([P, M], U8, name=f"w4_t{h}", align_bytes=64) for h in range(2)]
+        w4_s = keep.tile([P, M], U8, name="w4_s", align_bytes=64)
+        w_rows = keep.tile([P, P], F32, name="w_rows")
+        b_rows = keep.tile([P, P], F32, name="b_rows")
+        head_cols = keep.tile([P, S // P, P], F32, name="head_cols")
+        b_cols = keep.tile([P, NB], F32, name="b_cols")
+        ident = keep.tile([P, P], F32, name="ident")
+        warm = keep.tile([P, 1], F32, name="warm")
+        zero = keep.tile([P, 1], F32, name="zero")
+
+        xv = xT.rearrange("(p j) t -> p j t", j=PACK)
+        cv = c.rearrange("(p j) s -> p j s", j=PACK)
+        uv = u.rearrange("(p j) n -> p j n", j=PACK)
+
+        nc.gpsimd.memset(w_rows[32:64, :], 0.0)
+        nc.gpsimd.memset(w_rows[64:P, :], 0.0)
+        nc.vector.memset(b_rows[:], 0.0)
+        nc.vector.memset(zero[:], 0.0)
+        nc.vector.memset(w4_s[:].bitcast(I32), 0)
+        make_identity(nc, ident[:])
+
+        nc.sync.dma_start(offsets[:], offs)
+        nc.sync.dma_start(w_rows[0:32, :], wgt.rearrange("(g i) (q m) -> g q i m", i=P // HEADS, m=P)[:, :, 0, :])
+        nc.scalar.dma_start(b_rows[0:NB, :], b.rearrange("(t m) -> t m", m=P))
+        for q in range(4):
+            nc.scalar.dma_start(
+                w4_s[32 * q : 32 * q + 4, :].bitcast(I32), w4_scales[0, 4 * q : 4 * q + 4, :].bitcast(I32)
+            )
+        nc.sync.dma_start(planes[0][:], xv[:, 0, :])
+        nc.sync.dma_start(planes[1][:], xv[:, 1, :])
+        nc.sync.dma_start(planes[2][:], xv[:, 2, :])
+        nc.sync.dma_start(w4_t[0][:], w4_words[0, :, 0:M])
+        nc.sync.dma_start(planes[3][:], xv[:, 3, :])
+        nc.sync.dma_start(c_raw[:], cv)
+        nc.sync.dma_start(u_raw[0][:], uv[:, :, U_STARTS[0] : U_STARTS[0] + U_WIDTHS[0]])
+        nc.sync.dma_start(u_raw[1][:], uv[:, :, U_STARTS[1] : U_STARTS[1] + U_WIDTHS[1]])
+        nc.sync.dma_start(u_raw[2][:], uv[:, :, U_STARTS[2] : U_STARTS[2] + U_WIDTHS[2]])
+        nc.sync.dma_start(u_raw[3][:], uv[:, :, U_STARTS[3] : U_STARTS[3] + U_WIDTHS[3]])
+        nc.sync.dma_start(u_raw[4][:], uv[:, :, U_STARTS[4] : U_STARTS[4] + U_WIDTHS[4]])
+        nc.sync.dma_start(w4_t[1][:], w4_words[0, :, M : 2 * M])
+
+        nc.scalar.activation(warm[:], zero[:], IDENTITY)
+        turned = psum.tile([P, P], F32, name="turned", tag="acc6")
+        nc.tensor.transpose(turned[:], w_rows[:], ident[:])
+        nc.vector.tensor_copy(
+            head_cols[:].rearrange("p q (g i) -> p q g i", g=HEADS),
+            turned[:, 0:32].rearrange("p (g q) -> p q g", g=HEADS).unsqueeze(3).to_broadcast([P, S // P, HEADS, P // HEADS]),
+        )
+        spread = psum.tile([P, S], F32, name="spread", tag="acc5")
+        for q in range(S // P):
+            nc.tensor.transpose(spread[:, q * P : (q + 1) * P], head_cols[:, q, :], ident[:])
+        nc.scalar.copy(weights[:], spread[:])
+        b_ps = psum.tile([P, P], F32, name="b_ps", tag="acc7")
+        nc.tensor.transpose(b_ps[:], b_rows[:], ident[:])
+        nc.scalar.copy(b_cols[:], b_ps[:, 0:NB])
+
+        c_bf = keep.tile([P, S, PACK], BF16, name="c_bf", align_bytes=64)
+        c_codes = keep.tile([P, S], U32, name="c_codes", align_bytes=64)
+        c_scales = keep.tile([P, S], U8, name="c_scales", align_bytes=64)
+        g = [keep.tile([P, PACK, hi - lo], F32, name=f"g{lo}") for lo, hi in zip(G_CUTS, G_CUTS[1:])]
+        u_bf = [keep.tile([P, w, PACK], BF16, name=f"u_bf{q}", align_bytes=64) for q, w in enumerate(U_WIDTHS)]
+        u_codes = [keep.tile([P, w], U32, name=f"u_codes{q}", align_bytes=64) for q, w in enumerate(U_WIDTHS)]
+        u_scales = [keep.tile([P, w], U8, name=f"u_scales{q}", align_bytes=64) for q, w in enumerate(U_WIDTHS)]
+        xg_bf = keep.tile([P, S, PACK], BF16, name="xg_bf", align_bytes=64)
+        xg_codes = keep.tile([P, S], U32, name="xg_codes", align_bytes=64)
+        xg_scales = keep.tile([P, S], U8, name="xg_scales", align_bytes=64)
+        res = [keep.tile([P, S], F32, name=f"res{n}") for n in range(NB)]
+
+        def lay(engine, dst, src):
+            (nc.scalar.copy if engine == "S" else nc.vector.tensor_copy)(
+                dst.rearrange("p (r i) j -> p r j i", i=4), src.rearrange("p j (r i) -> p r j i", i=4)
+            )
+
+        def quant(codes, scales, src):
+            nc.vector.quantize_mx(out=codes.bitcast(E4M3X4), scales=scales, in_=src.rearrange("p w j -> p (w j)"))
+
+        for pair, pair_on in ((0, PAIR0_ON), (1, PAIR1_ON)):
+            both = slice(2 * pair, 2 * pair + 2)
+            for i in (2 * pair, 2 * pair + 1):
+                for h, (lo, hi) in enumerate(zip(G_CUTS, G_CUTS[1:])):
+                    nc.vector.tensor_tensor(
+                        g[h][:, i, :], planes[i][:].indirect(offsets[:, lo // 16 : hi // 16]), weights[:, lo:hi], MULT
+                    )
+            for h, (lo, hi) in enumerate(zip(G_CUTS, G_CUTS[1:])):
+                lay(pair_on[h], xg_bf[:, lo:hi, both], g[h][:, both, :])
+
+        lay("S", c_bf[:, 0:C_SCALAR, :], c_raw[:, :, 0:C_SCALAR])
+        lay("V", c_bf[:, C_SCALAR:S, :], c_raw[:, :, C_SCALAR:S])
+        quant(c_codes[:], c_scales[:], c_bf[:])
+        quant(xg_codes[:], xg_scales[:], xg_bf[:])
+        accs = [psum.tile([P, S], F32, name=f"acc{n}", tag=f"acc{n}") for n in range(NB)]
+
+        def w_pass(n, start):
+            h, k = divmod(2 * P * n, M)
+            nc.tensor.matmul_mx(
+                out=accs[n][:],
+                lhsT=w4_t[h][:, k : k + 2 * P].bitcast(E2M1X4),
+                lhsT_scale=w4_s[:, P * n : P * (n + 1)],
+                rhs=xg_codes[:].bitcast(E4M3X4),
+                rhs_scale=xg_scales[:],
+                start=start,
+                stop=not start,
+            )
+
+        def u_pass(n, q, k, start):
+            nc.tensor.matmul_mx(
+                out=accs[n][:],
+                lhsT=u_codes[q][:, k : k + P].bitcast(E4M3X4),
+                lhsT_scale=u_scales[q][:, k : k + P],
+                rhs=c_codes[:].bitcast(E4M3X4),
+                rhs_scale=c_scales[:],
+                start=start,
+                stop=not start,
+            )
+
+        def finish(n):
+            if DRAIN_ON[n] == "S":
+                nc.scalar.activation(res[n][:], accs[n][:], IDENTITY, bias=b_cols[:, n : n + 1])
+            else:
+                nc.vector.tensor_scalar(res[n][:], accs[n][:], b_cols[:, n : n + 1], None, ADD)
+            nc.sync.dma_start(out[n * P : (n + 1) * P, :], res[n][:])
+
+        for q, (u0, w) in enumerate(zip(U_STARTS, U_WIDTHS)):
+            cut = U_SCALAR[q]
+            if cut > 0:
+                lay("S", u_bf[q][:, 0:cut, :], u_raw[q][:, :, 0:cut])
+            if cut < w:
+                lay("V", u_bf[q][:, cut:w, :], u_raw[q][:, :, cut:w])
+            quant(u_codes[q][:], u_scales[q][:], u_bf[q][:])
+            for k in range(0, w, P):
+                n = (u0 + k) // P
+                if n < NB // 2:
+                    w_pass(n, True)
+                    u_pass(n, q, k, False)
+                else:
+                    u_pass(n, q, k, True)
+                    w_pass(n, False)
+                finish(n)

@@ -20,14 +20,9 @@ PACK = 4
 K, L, M, T, S = 512, 512, 1024, 2048, 512
 NB = M // P
 HEADS = 8
-U_WIDTHS = (256, 256, 256, 128, 128,)
-U_STARTS = (0, 256, 512, 768, 896,)
-U_SCALAR = (0, 192, 64, 0, 64,)
-C_SCALAR = 256
-G_CUTS = (0, 320, 512)
-PAIR0_ON = "VV"
-PAIR1_ON = "VS"
-DRAIN_ON = "SSSVVVSV"
+HALF = S // 2
+U_W = 256
+NU = M // U_W
 
 FLOPS = 2 * M * S * (K + L)
 
@@ -42,7 +37,7 @@ def tile_list_hmix_bias_kernel(tc, xT, w4_words, w4_scales, c, u, wgt, b, offs, 
         weights = keep.tile([P, S], F32, name="weights")
         planes = [keep.tile([P, T], F32, name=f"plane{i}") for i in range(PACK)]
         c_raw = keep.tile([P, PACK, S], F32, name="c_raw")
-        u_raw = [keep.tile([P, PACK, w], F32, name=f"u_raw{q}") for q, w in enumerate(U_WIDTHS)]
+        u_raw = [keep.tile([P, PACK, U_W], F32, name=f"u_raw{q}") for q in range(NU)]
         w4_t = [keep.tile([P, M], U8, name=f"w4_t{h}", align_bytes=64) for h in range(2)]
         w4_s = keep.tile([P, M], U8, name="w4_s", align_bytes=64)
         w_rows = keep.tile([P, P], F32, name="w_rows")
@@ -57,31 +52,27 @@ def tile_list_hmix_bias_kernel(tc, xT, w4_words, w4_scales, c, u, wgt, b, offs, 
         cv = c.rearrange("(p j) s -> p j s", j=PACK)
         uv = u.rearrange("(p j) n -> p j n", j=PACK)
 
-        nc.gpsimd.memset(w_rows[32:64, :], 0.0)
-        nc.gpsimd.memset(w_rows[64:P, :], 0.0)
-        nc.vector.memset(b_rows[:], 0.0)
+        nc.gpsimd.memset(w4_s[:].bitcast(I32), 0)
+        nc.gpsimd.memset(b_rows[:], 0.0)
+        nc.vector.memset(w_rows[32:64, :], 0.0)
+        nc.vector.memset(w_rows[64:P, :], 0.0)
         nc.vector.memset(zero[:], 0.0)
-        nc.vector.memset(w4_s[:].bitcast(I32), 0)
         make_identity(nc, ident[:])
 
-        nc.sync.dma_start(offsets[:], offs)
         nc.sync.dma_start(w_rows[0:32, :], wgt.rearrange("(g i) (q m) -> g q i m", i=P // HEADS, m=P)[:, :, 0, :])
+        nc.sync.dma_start(planes[0][:], xv[:, 0, :])
+        nc.sync.dma_start(offsets[:], offs)
         nc.scalar.dma_start(b_rows[0:NB, :], b.rearrange("(t m) -> t m", m=P))
         for q in range(4):
             nc.scalar.dma_start(
                 w4_s[32 * q : 32 * q + 4, :].bitcast(I32), w4_scales[0, 4 * q : 4 * q + 4, :].bitcast(I32)
             )
-        nc.sync.dma_start(planes[0][:], xv[:, 0, :])
-        nc.sync.dma_start(planes[1][:], xv[:, 1, :])
-        nc.sync.dma_start(planes[2][:], xv[:, 2, :])
-        nc.sync.dma_start(w4_t[0][:], w4_words[0, :, 0:M])
-        nc.sync.dma_start(planes[3][:], xv[:, 3, :])
+        for i in range(1, PACK):
+            nc.sync.dma_start(planes[i][:], xv[:, i, :])
         nc.sync.dma_start(c_raw[:], cv)
-        nc.sync.dma_start(u_raw[0][:], uv[:, :, U_STARTS[0] : U_STARTS[0] + U_WIDTHS[0]])
-        nc.sync.dma_start(u_raw[1][:], uv[:, :, U_STARTS[1] : U_STARTS[1] + U_WIDTHS[1]])
-        nc.sync.dma_start(u_raw[2][:], uv[:, :, U_STARTS[2] : U_STARTS[2] + U_WIDTHS[2]])
-        nc.sync.dma_start(u_raw[3][:], uv[:, :, U_STARTS[3] : U_STARTS[3] + U_WIDTHS[3]])
-        nc.sync.dma_start(u_raw[4][:], uv[:, :, U_STARTS[4] : U_STARTS[4] + U_WIDTHS[4]])
+        nc.sync.dma_start(w4_t[0][:], w4_words[0, :, 0:M])
+        for q in range(NU):
+            nc.sync.dma_start(u_raw[q][:], uv[:, :, q * U_W : (q + 1) * U_W])
         nc.sync.dma_start(w4_t[1][:], w4_words[0, :, M : 2 * M])
 
         nc.scalar.activation(warm[:], zero[:], IDENTITY)
@@ -102,10 +93,12 @@ def tile_list_hmix_bias_kernel(tc, xT, w4_words, w4_scales, c, u, wgt, b, offs, 
         c_bf = keep.tile([P, S, PACK], BF16, name="c_bf", align_bytes=64)
         c_codes = keep.tile([P, S], U32, name="c_codes", align_bytes=64)
         c_scales = keep.tile([P, S], U8, name="c_scales", align_bytes=64)
-        g = [keep.tile([P, PACK, hi - lo], F32, name=f"g{lo}") for lo, hi in zip(G_CUTS, G_CUTS[1:])]
-        u_bf = [keep.tile([P, w, PACK], BF16, name=f"u_bf{q}", align_bytes=64) for q, w in enumerate(U_WIDTHS)]
-        u_codes = [keep.tile([P, w], U32, name=f"u_codes{q}", align_bytes=64) for q, w in enumerate(U_WIDTHS)]
-        u_scales = [keep.tile([P, w], U8, name=f"u_scales{q}", align_bytes=64) for q, w in enumerate(U_WIDTHS)]
+        g_early = keep.tile([P, 2, S], F32, name="g_early")
+        g_late = [keep.tile([P, 2, HALF], F32, name=f"g_late{h}") for h in range(2)]
+        u_bf = [keep.tile([P, P, PACK], BF16, name=f"u_bf{n}", align_bytes=64) for n in range(2)]
+        u_bf = u_bf + [keep.tile([P, U_W, PACK], BF16, name=f"u_bfw{q}", align_bytes=64) for q in range(1, NU)]
+        u_codes = keep.tile([P, M], U32, name="u_codes", align_bytes=64)
+        u_scales = keep.tile([P, M], U8, name="u_scales", align_bytes=64)
         xg_bf = keep.tile([P, S, PACK], BF16, name="xg_bf", align_bytes=64)
         xg_codes = keep.tile([P, S], U32, name="xg_codes", align_bytes=64)
         xg_scales = keep.tile([P, S], U8, name="xg_scales", align_bytes=64)
@@ -119,20 +112,22 @@ def tile_list_hmix_bias_kernel(tc, xT, w4_words, w4_scales, c, u, wgt, b, offs, 
         def quant(codes, scales, src):
             nc.vector.quantize_mx(out=codes.bitcast(E4M3X4), scales=scales, in_=src.rearrange("p w j -> p (w j)"))
 
-        for pair, pair_on in ((0, PAIR0_ON), (1, PAIR1_ON)):
-            both = slice(2 * pair, 2 * pair + 2)
-            for i in (2 * pair, 2 * pair + 1):
-                for h, (lo, hi) in enumerate(zip(G_CUTS, G_CUTS[1:])):
-                    nc.vector.tensor_tensor(
-                        g[h][:, i, :], planes[i][:].indirect(offsets[:, lo // 16 : hi // 16]), weights[:, lo:hi], MULT
-                    )
-            for h, (lo, hi) in enumerate(zip(G_CUTS, G_CUTS[1:])):
-                lay(pair_on[h], xg_bf[:, lo:hi, both], g[h][:, both, :])
-
-        lay("S", c_bf[:, 0:C_SCALAR, :], c_raw[:, :, 0:C_SCALAR])
-        lay("V", c_bf[:, C_SCALAR:S, :], c_raw[:, :, C_SCALAR:S])
-        quant(c_codes[:], c_scales[:], c_bf[:])
+        for i in range(2):
+            nc.vector.tensor_tensor(g_early[:, i, :], planes[i][:].indirect(offsets[:]), weights[:], MULT)
+        lay("S", xg_bf[:, :, 0:2], g_early[:])
+        for i in range(2):
+            for h in range(2):
+                lo, hi = h * HALF, (h + 1) * HALF
+                nc.vector.tensor_tensor(
+                    g_late[h][:, i, :], planes[2 + i][:].indirect(offsets[:, lo // 16 : hi // 16]), weights[:, lo:hi], MULT
+                )
+        lay("S", xg_bf[:, 0:HALF, 2:4], g_late[0][:])
+        lay("V", xg_bf[:, HALF:S, 2:4], g_late[1][:])
         quant(xg_codes[:], xg_scales[:], xg_bf[:])
+
+        lay("S", c_bf[:, 0:192, :], c_raw[:, :, 0:192])
+        lay("V", c_bf[:, 192:S, :], c_raw[:, :, 192:S])
+        quant(c_codes[:], c_scales[:], c_bf[:])
         accs = [psum.tile([P, S], F32, name=f"acc{n}", tag=f"acc{n}") for n in range(NB)]
 
         def w_pass(n, start):
@@ -147,11 +142,11 @@ def tile_list_hmix_bias_kernel(tc, xT, w4_words, w4_scales, c, u, wgt, b, offs, 
                 stop=not start,
             )
 
-        def u_pass(n, q, k, start):
+        def u_pass(n, start):
             nc.tensor.matmul_mx(
                 out=accs[n][:],
-                lhsT=u_codes[q][:, k : k + P].bitcast(E4M3X4),
-                lhsT_scale=u_scales[q][:, k : k + P],
+                lhsT=u_codes[:, P * n : P * (n + 1)].bitcast(E4M3X4),
+                lhsT_scale=u_scales[:, P * n : P * (n + 1)],
                 rhs=c_codes[:].bitcast(E4M3X4),
                 rhs_scale=c_scales[:],
                 start=start,
@@ -159,25 +154,29 @@ def tile_list_hmix_bias_kernel(tc, xT, w4_words, w4_scales, c, u, wgt, b, offs, 
             )
 
         def finish(n):
-            if DRAIN_ON[n] == "S":
+            if n != NB - 2:
                 nc.scalar.activation(res[n][:], accs[n][:], IDENTITY, bias=b_cols[:, n : n + 1])
             else:
                 nc.vector.tensor_scalar(res[n][:], accs[n][:], b_cols[:, n : n + 1], None, ADD)
             nc.sync.dma_start(out[n * P : (n + 1) * P, :], res[n][:])
 
-        for q, (u0, w) in enumerate(zip(U_STARTS, U_WIDTHS)):
-            cut = U_SCALAR[q]
-            if cut > 0:
-                lay("S", u_bf[q][:, 0:cut, :], u_raw[q][:, :, 0:cut])
-            if cut < w:
-                lay("V", u_bf[q][:, cut:w, :], u_raw[q][:, :, cut:w])
-            quant(u_codes[q][:], u_scales[q][:], u_bf[q][:])
-            for k in range(0, w, P):
-                n = (u0 + k) // P
+        for n in range(NB // 2):
+            w_pass(n, True)
+        for n in range(2):
+            cols = slice(n * P, (n + 1) * P)
+            lay("S", u_bf[n][:], u_raw[0][:, :, cols])
+            quant(u_codes[:, cols], u_scales[:, cols], u_bf[n][:])
+            u_pass(n, False)
+        for n in range(2):
+            finish(n)
+        for q in range(1, NU):
+            cols = slice(q * U_W, (q + 1) * U_W)
+            lay("V", u_bf[1 + q][:], u_raw[q][:])
+            quant(u_codes[:, cols], u_scales[:, cols], u_bf[1 + q][:])
+            for n in (2 * q, 2 * q + 1):
                 if n < NB // 2:
-                    w_pass(n, True)
-                    u_pass(n, q, k, False)
+                    u_pass(n, False)
                 else:
-                    u_pass(n, q, k, True)
+                    u_pass(n, True)
                     w_pass(n, False)
                 finish(n)

@@ -21,8 +21,11 @@ K, L, M, T, S = 512, 512, 1024, 2048, 512
 NB = M // P
 HEADS = 8
 HALF = S // 2
-U_W = 256
-NU = M // U_W
+W_FIRST = 3
+G_PARTS = ((0, HALF), (HALF, S))
+U_CUTS = (0, 128, 384, 640, 896, 1024)
+U_PARTS = tuple(zip(U_CUTS, U_CUTS[1:]))
+U_OPENS = ()
 
 FLOPS = 2 * M * S * (K + L)
 
@@ -36,9 +39,9 @@ def tile_list_hmix_bias_kernel(tc, xT, w4_words, w4_scales, c, u, wgt, b, offs, 
         offsets = keep.tile([P, S // 16], U16, name="offsets")
         weights = keep.tile([P, S], F32, name="weights")
         planes = [keep.tile([P, T], F32, name=f"plane{i}") for i in range(PACK)]
-        c_raw = keep.tile([P, PACK, S], F32, name="c_raw")
-        u_raw = [keep.tile([P, PACK, U_W], F32, name=f"u_raw{q}") for q in range(NU)]
-        w4_t = [keep.tile([P, M], U8, name=f"w4_t{h}", align_bytes=64) for h in range(2)]
+        c_raw = [keep.tile([P, PACK, HALF], F32, name=f"c_raw{h}") for h in range(2)]
+        u_raw = [keep.tile([P, PACK, hi - lo], F32, name=f"u_raw{lo}", tag=f"u_raw{lo}", align_bytes=64) for lo, hi in U_PARTS]
+        w4_t = [keep.tile([P, 2 * P * nb], U8, name=f"w4_t{h}", align_bytes=64) for h, nb in enumerate((W_FIRST, NB - W_FIRST))]
         w4_s = keep.tile([P, M], U8, name="w4_s", align_bytes=64)
         w_rows = keep.tile([P, P], F32, name="w_rows")
         b_rows = keep.tile([P, P], F32, name="b_rows")
@@ -58,6 +61,11 @@ def tile_list_hmix_bias_kernel(tc, xT, w4_words, w4_scales, c, u, wgt, b, offs, 
         nc.vector.memset(w_rows[64:P, :], 0.0)
         nc.vector.memset(zero[:], 0.0)
         make_identity(nc, ident[:])
+        zeros = keep.tile([P, S * PACK], BF16, name="zeros", align_bytes=64)
+        warm_codes = keep.tile([P, S], U32, name="warm_codes", align_bytes=64)
+        warm_scales = keep.tile([P, S], U8, name="warm_scales", align_bytes=64)
+        nc.gpsimd.memset(zeros[:].bitcast(U32), 0)
+        nc.vector.quantize_mx(out=warm_codes[:].bitcast(E4M3X4), scales=warm_scales[:], in_=zeros[:])
 
         nc.sync.dma_start(w_rows[0:32, :], wgt.rearrange("(g i) (q m) -> g q i m", i=P // HEADS, m=P)[:, :, 0, :])
         nc.sync.dma_start(planes[0][:], xv[:, 0, :])
@@ -69,11 +77,13 @@ def tile_list_hmix_bias_kernel(tc, xT, w4_words, w4_scales, c, u, wgt, b, offs, 
             )
         for i in range(1, PACK):
             nc.sync.dma_start(planes[i][:], xv[:, i, :])
-        nc.sync.dma_start(c_raw[:], cv)
-        nc.sync.dma_start(w4_t[0][:], w4_words[0, :, 0:M])
-        for q in range(NU):
-            nc.sync.dma_start(u_raw[q][:], uv[:, :, q * U_W : (q + 1) * U_W])
-        nc.sync.dma_start(w4_t[1][:], w4_words[0, :, M : 2 * M])
+        nc.sync.dma_start(c_raw[0][:], cv[:, :, 0:HALF])
+        nc.sync.dma_start(w4_t[0][:], w4_words[0, :, 0 : 2 * P * W_FIRST])
+        nc.sync.dma_start(c_raw[1][:], cv[:, :, HALF:S])
+        for q, (lo, hi) in enumerate(U_PARTS):
+            nc.sync.dma_start(u_raw[q][:], uv[:, :, lo:hi])
+            if q == 2:
+                nc.sync.dma_start(w4_t[1][:], w4_words[0, :, 2 * P * W_FIRST : 2 * M])
 
         nc.scalar.activation(warm[:], zero[:], IDENTITY)
         turned = psum.tile([P, P], F32, name="turned", tag="acc6")
@@ -90,19 +100,17 @@ def tile_list_hmix_bias_kernel(tc, xT, w4_words, w4_scales, c, u, wgt, b, offs, 
         nc.tensor.transpose(b_ps[:], b_rows[:], ident[:])
         nc.scalar.copy(b_cols[:], b_ps[:, 0:NB])
 
-        c_bf = keep.tile([P, S, PACK], BF16, name="c_bf", align_bytes=64)
+        c_bf = [keep.tile([P, HALF, PACK], BF16, name=f"c_bf{h}", align_bytes=64) for h in range(2)]
         c_codes = keep.tile([P, S], U32, name="c_codes", align_bytes=64)
         c_scales = keep.tile([P, S], U8, name="c_scales", align_bytes=64)
         g_early = keep.tile([P, 2, S], F32, name="g_early")
-        g_late = [keep.tile([P, 2, HALF], F32, name=f"g_late{h}") for h in range(2)]
-        u_bf = [keep.tile([P, P, PACK], BF16, name=f"u_bf{n}", align_bytes=64) for n in range(2)]
-        u_bf = u_bf + [keep.tile([P, U_W, PACK], BF16, name=f"u_bfw{q}", align_bytes=64) for q in range(1, NU)]
+        g_late = [keep.tile([P, 2, hi - lo], F32, name=f"g_late{lo}") for lo, hi in G_PARTS]
+        u_bf = [keep.tile([P, P, PACK], BF16, name=f"u_bf{n}", tag=f"u_bf{n}", align_bytes=64) for n in range(NB)]
         u_codes = keep.tile([P, M], U32, name="u_codes", align_bytes=64)
         u_scales = keep.tile([P, M], U8, name="u_scales", align_bytes=64)
-        xg_bf = keep.tile([P, S, PACK], BF16, name="xg_bf", align_bytes=64)
+        xg_bf = [keep.tile([P, HALF, PACK], BF16, name=f"xg_bf{h}", align_bytes=64) for h in range(2)]
         xg_codes = keep.tile([P, S], U32, name="xg_codes", align_bytes=64)
         xg_scales = keep.tile([P, S], U8, name="xg_scales", align_bytes=64)
-        res = [keep.tile([P, S], F32, name=f"res{n}") for n in range(NB)]
 
         def lay(engine, dst, src):
             (nc.scalar.copy if engine == "S" else nc.vector.tensor_copy)(
@@ -114,24 +122,39 @@ def tile_list_hmix_bias_kernel(tc, xT, w4_words, w4_scales, c, u, wgt, b, offs, 
 
         for i in range(2):
             nc.vector.tensor_tensor(g_early[:, i, :], planes[i][:].indirect(offsets[:]), weights[:], MULT)
-        lay("S", xg_bf[:, :, 0:2], g_early[:])
+        halves = [slice(h * HALF, (h + 1) * HALF) for h in range(2)]
+        for h in range(2):
+            lay("S", xg_bf[h][:, :, 0:2], g_early[:, :, halves[h]])
         for i in range(2):
-            for h in range(2):
-                lo, hi = h * HALF, (h + 1) * HALF
+            for h, (lo, hi) in enumerate(G_PARTS):
                 nc.vector.tensor_tensor(
                     g_late[h][:, i, :], planes[2 + i][:].indirect(offsets[:, lo // 16 : hi // 16]), weights[:, lo:hi], MULT
                 )
-        lay("S", xg_bf[:, 0:HALF, 2:4], g_late[0][:])
-        lay("V", xg_bf[:, HALF:S, 2:4], g_late[1][:])
-        quant(xg_codes[:], xg_scales[:], xg_bf[:])
-
-        lay("S", c_bf[:, 0:192, :], c_raw[:, :, 0:192])
-        lay("V", c_bf[:, 192:S, :], c_raw[:, :, 192:S])
-        quant(c_codes[:], c_scales[:], c_bf[:])
+        for part, (lo, hi) in enumerate(G_PARTS):
+            h = lo // HALF
+            lay("V", xg_bf[h][:, lo - h * HALF : hi - h * HALF, 2:4], g_late[part][:])
+        for h in range(2):
+            quant(xg_codes[:, halves[h]], xg_scales[:, halves[h]], xg_bf[h][:])
+        for h in range(2):
+            lay("S", c_bf[h][:], c_raw[h][:])
+        for h in range(2):
+            quant(c_codes[:, halves[h]], c_scales[:, halves[h]], c_bf[h][:])
+        warm_ps = psum.tile([P, S], F32, name="warm_ps", tag="acc7")
+        for width in (S, HALF):
+            nc.tensor.matmul_mx(
+                out=warm_ps[:, 0:width],
+                lhsT=w4_t[0][:, 0 : 2 * P].bitcast(E2M1X4),
+                lhsT_scale=w4_s[:, 0:P],
+                rhs=warm_codes[:, 0:width].bitcast(E4M3X4),
+                rhs_scale=warm_scales[:, 0:width],
+                start=True,
+                stop=True,
+            )
         accs = [psum.tile([P, S], F32, name=f"acc{n}", tag=f"acc{n}") for n in range(NB)]
 
         def w_pass(n, start):
-            h, k = divmod(2 * P * n, M)
+            h = 0 if n < W_FIRST else 1
+            k = 2 * P * (n - h * W_FIRST)
             nc.tensor.matmul_mx(
                 out=accs[n][:],
                 lhsT=w4_t[h][:, k : k + 2 * P].bitcast(E2M1X4),
@@ -154,29 +177,38 @@ def tile_list_hmix_bias_kernel(tc, xT, w4_words, w4_scales, c, u, wgt, b, offs, 
             )
 
         def finish(n):
+            tag = {0: f"u_raw{U_CUTS[1]}", NB - 2: f"u_bf{NB - 1}"}.get(n, f"res{n}")
+            res = keep.tile([P, S], F32, name=f"res{n}", tag=tag, align_bytes=64)
             if n != NB - 2:
-                nc.scalar.activation(res[n][:], accs[n][:], IDENTITY, bias=b_cols[:, n : n + 1])
+                nc.scalar.activation(res[:], accs[n][:], IDENTITY, bias=b_cols[:, n : n + 1])
             else:
-                nc.vector.tensor_scalar(res[n][:], accs[n][:], b_cols[:, n : n + 1], None, ADD)
-            nc.sync.dma_start(out[n * P : (n + 1) * P, :], res[n][:])
+                nc.vector.tensor_scalar(res[:], accs[n][:], b_cols[:, n : n + 1], None, ADD)
+            nc.sync.dma_start(out[n * P : (n + 1) * P, :], res[:])
 
-        for n in range(NB // 2):
-            w_pass(n, True)
-        for n in range(2):
-            cols = slice(n * P, (n + 1) * P)
-            lay("S", u_bf[n][:], u_raw[0][:, :, cols])
-            quant(u_codes[:, cols], u_scales[:, cols], u_bf[n][:])
-            u_pass(n, False)
-        for n in range(2):
-            finish(n)
-        for q in range(1, NU):
-            cols = slice(q * U_W, (q + 1) * U_W)
-            lay("V", u_bf[1 + q][:], u_raw[q][:])
-            quant(u_codes[:, cols], u_scales[:, cols], u_bf[1 + q][:])
-            for n in (2 * q, 2 * q + 1):
-                if n < NB // 2:
-                    u_pass(n, False)
-                else:
+        def lay_u(engine, n):
+            q = max(i for i, (lo, hi) in enumerate(U_PARTS) if lo <= n * P)
+            k = n * P - U_CUTS[q]
+            lay(engine, u_bf[n][:], u_raw[q][:, :, k : k + P])
+
+        def quant_u(n):
+            quant(u_codes[:, n * P : (n + 1) * P], u_scales[:, n * P : (n + 1) * P], u_bf[n][:])
+
+        def banks(first, last):
+            for n in range(first, last):
+                if n in U_OPENS:
                     u_pass(n, True)
                     w_pass(n, False)
+                else:
+                    if n >= W_FIRST:
+                        w_pass(n, True)
+                    u_pass(n, False)
                 finish(n)
+
+        for n in range(W_FIRST):
+            w_pass(n, True)
+        for lo, hi in U_PARTS:
+            for n in range(lo // P, hi // P):
+                lay_u("S" if n == 1 else "V", n)
+            for n in range(lo // P, hi // P):
+                quant_u(n)
+        banks(0, NB)

@@ -61,11 +61,6 @@ def tile_list_hmix_bias_kernel(tc, xT, w4_words, w4_scales, c, u, wgt, b, offs, 
         nc.vector.memset(w_rows[64:P, :], 0.0)
         nc.vector.memset(zero[:], 0.0)
         make_identity(nc, ident[:])
-        zeros = keep.tile([P, S * PACK], BF16, name="zeros", align_bytes=64)
-        warm_codes = keep.tile([P, S], U32, name="warm_codes", align_bytes=64)
-        warm_scales = keep.tile([P, S], U8, name="warm_scales", align_bytes=64)
-        nc.gpsimd.memset(zeros[:].bitcast(U32), 0)
-        nc.vector.quantize_mx(out=warm_codes[:].bitcast(E4M3X4), scales=warm_scales[:], in_=zeros[:])
 
         nc.sync.dma_start(w_rows[0:32, :], wgt.rearrange("(g i) (q m) -> g q i m", i=P // HEADS, m=P)[:, :, 0, :])
         nc.sync.dma_start(planes[0][:], xv[:, 0, :])
@@ -139,17 +134,6 @@ def tile_list_hmix_bias_kernel(tc, xT, w4_words, w4_scales, c, u, wgt, b, offs, 
             lay("S", c_bf[h][:], c_raw[h][:])
         for h in range(2):
             quant(c_codes[:, halves[h]], c_scales[:, halves[h]], c_bf[h][:])
-        warm_ps = psum.tile([P, S], F32, name="warm_ps", tag="acc7")
-        for width in (S, HALF):
-            nc.tensor.matmul_mx(
-                out=warm_ps[:, 0:width],
-                lhsT=w4_t[0][:, 0 : 2 * P].bitcast(E2M1X4),
-                lhsT_scale=w4_s[:, 0:P],
-                rhs=warm_codes[:, 0:width].bitcast(E4M3X4),
-                rhs_scale=warm_scales[:, 0:width],
-                start=True,
-                stop=True,
-            )
         accs = [psum.tile([P, S], F32, name=f"acc{n}", tag=f"acc{n}") for n in range(NB)]
 
         def w_pass(n, start):

@@ -18,14 +18,15 @@ IDENTITY = mybir.ActivationFunctionType.Identity
 P = 128
 PACK = 4
 K, L, M, T, S = 512, 512, 1024, 2048, 512
-NB = M // P
 HEADS = 8
+GROUP = P // HEADS
+BANDS = M // P
 HALF = S // 2
-W_FIRST = 3
-G_PARTS = ((0, HALF), (HALF, S))
-U_CUTS = (0, 128, 384, 640, 896, 1024)
-U_PARTS = tuple(zip(U_CUTS, U_CUTS[1:]))
-U_OPENS = ()
+HALVES = (slice(0, HALF), slice(HALF, S))
+U_PIECES = ((0,), (1, 2), (3, 4), (5, 6), (7,))
+EARLY = 3
+SCALAR_WEAVES = 1
+VECTOR_EMPTIES = BANDS - 2
 
 FLOPS = 2 * M * S * (K + L)
 
@@ -36,163 +37,148 @@ def tile_list_hmix_bias_kernel(tc, xT, w4_words, w4_scales, c, u, wgt, b, offs, 
         keep = ctx.enter_context(tc.tile_pool(name="keep", bufs=1))
         psum = ctx.enter_context(tc.psum_pool(name="psum", bufs=1))
 
-        offsets = keep.tile([P, S // 16], U16, name="offsets")
+        offsets = keep.tile([P, S // GROUP], U16, name="offsets")
         weights = keep.tile([P, S], F32, name="weights")
         planes = [keep.tile([P, T], F32, name=f"plane{i}") for i in range(PACK)]
         c_raw = [keep.tile([P, PACK, HALF], F32, name=f"c_raw{h}") for h in range(2)]
-        u_raw = [keep.tile([P, PACK, hi - lo], F32, name=f"u_raw{lo}", tag=f"u_raw{lo}", align_bytes=64) for lo, hi in U_PARTS]
-        w4_t = [keep.tile([P, 2 * P * nb], U8, name=f"w4_t{h}", align_bytes=64) for h, nb in enumerate((W_FIRST, NB - W_FIRST))]
-        w4_s = keep.tile([P, M], U8, name="w4_s", align_bytes=64)
-        w_rows = keep.tile([P, P], F32, name="w_rows")
+        u_raw = [
+            keep.tile([P, PACK, P * len(piece)], F32, name=f"u_raw{q}", tag=f"u_raw{q}", align_bytes=64)
+            for q, piece in enumerate(U_PIECES)
+        ]
+        w4_early = keep.tile([P, 2 * P * EARLY], U8, name="w4_early", align_bytes=64)
+        w4_late = keep.tile([P, 2 * P * (BANDS - EARLY)], U8, name="w4_late", align_bytes=64)
+        w4_scale_rows = keep.tile([P, M], U8, name="w4_scale_rows", align_bytes=64)
+        wgt_rows = keep.tile([P, P], F32, name="wgt_rows")
         b_rows = keep.tile([P, P], F32, name="b_rows")
-        head_cols = keep.tile([P, S // P, P], F32, name="head_cols")
-        b_cols = keep.tile([P, NB], F32, name="b_cols")
+        wgt_cols = keep.tile([P, S // P, P], F32, name="wgt_cols")
+        b_cols = keep.tile([P, BANDS], F32, name="b_cols")
         ident = keep.tile([P, P], F32, name="ident")
-        warm = keep.tile([P, 1], F32, name="warm")
-        zero = keep.tile([P, 1], F32, name="zero")
 
-        xv = xT.rearrange("(p j) t -> p j t", j=PACK)
-        cv = c.rearrange("(p j) s -> p j s", j=PACK)
-        uv = u.rearrange("(p j) n -> p j n", j=PACK)
+        xv = xT.rearrange("(p i) t -> p i t", i=PACK)
+        cv = c.rearrange("(p i) s -> p i s", i=PACK)
+        uv = u.rearrange("(p i) n -> p i n", i=PACK)
 
-        nc.gpsimd.memset(w4_s[:].bitcast(I32), 0)
+        nc.gpsimd.memset(w4_scale_rows[:].bitcast(I32), 0)
         nc.gpsimd.memset(b_rows[:], 0.0)
-        nc.vector.memset(w_rows[32:64, :], 0.0)
-        nc.vector.memset(w_rows[64:P, :], 0.0)
-        nc.vector.memset(zero[:], 0.0)
+        nc.vector.memset(wgt_rows[32:64, :], 0.0)
+        nc.vector.memset(wgt_rows[64:P, :], 0.0)
         make_identity(nc, ident[:])
 
-        nc.sync.dma_start(w_rows[0:32, :], wgt.rearrange("(g i) (q m) -> g q i m", i=P // HEADS, m=P)[:, :, 0, :])
+        nc.sync.dma_start(wgt_rows[0:32, :], wgt.rearrange("(g r) (q m) -> g q r m", r=GROUP, m=P)[:, :, 0, :])
         nc.sync.dma_start(planes[0][:], xv[:, 0, :])
         nc.sync.dma_start(offsets[:], offs)
-        nc.scalar.dma_start(b_rows[0:NB, :], b.rearrange("(t m) -> t m", m=P))
+        nc.scalar.dma_start(b_rows[0:BANDS, :], b.rearrange("(t m) -> t m", m=P))
         for q in range(4):
             nc.scalar.dma_start(
-                w4_s[32 * q : 32 * q + 4, :].bitcast(I32), w4_scales[0, 4 * q : 4 * q + 4, :].bitcast(I32)
+                w4_scale_rows[32 * q : 32 * q + 4, :].bitcast(I32), w4_scales[0, 4 * q : 4 * q + 4, :].bitcast(I32)
             )
         for i in range(1, PACK):
             nc.sync.dma_start(planes[i][:], xv[:, i, :])
-        nc.sync.dma_start(c_raw[0][:], cv[:, :, 0:HALF])
-        nc.sync.dma_start(w4_t[0][:], w4_words[0, :, 0 : 2 * P * W_FIRST])
-        nc.sync.dma_start(c_raw[1][:], cv[:, :, HALF:S])
-        for q, (lo, hi) in enumerate(U_PARTS):
-            nc.sync.dma_start(u_raw[q][:], uv[:, :, lo:hi])
-            if q == 2:
-                nc.sync.dma_start(w4_t[1][:], w4_words[0, :, 2 * P * W_FIRST : 2 * M])
+        nc.sync.dma_start(c_raw[0][:], cv[:, :, HALVES[0]])
+        nc.sync.dma_start(w4_early[:], w4_words[0, :, 0 : 2 * P * EARLY])
+        nc.sync.dma_start(c_raw[1][:], cv[:, :, HALVES[1]])
+        for q, piece in enumerate(U_PIECES):
+            nc.sync.dma_start(u_raw[q][:], uv[:, :, P * piece[0] : P * (piece[-1] + 1)])
+            if EARLY in piece:
+                nc.sync.dma_start(w4_late[:], w4_words[0, :, 2 * P * EARLY : 2 * M])
 
-        nc.scalar.activation(warm[:], zero[:], IDENTITY)
         turned = psum.tile([P, P], F32, name="turned", tag="acc6")
-        nc.tensor.transpose(turned[:], w_rows[:], ident[:])
+        nc.tensor.transpose(turned[:], wgt_rows[:], ident[:])
         nc.vector.tensor_copy(
-            head_cols[:].rearrange("p q (g i) -> p q g i", g=HEADS),
-            turned[:, 0:32].rearrange("p (g q) -> p q g", g=HEADS).unsqueeze(3).to_broadcast([P, S // P, HEADS, P // HEADS]),
+            wgt_cols[:].rearrange("m q (g r) -> m q g r", g=HEADS),
+            turned[:, 0:32].rearrange("m (g q) -> m q g", g=HEADS).unsqueeze(3).to_broadcast([P, S // P, HEADS, GROUP]),
         )
         spread = psum.tile([P, S], F32, name="spread", tag="acc5")
         for q in range(S // P):
-            nc.tensor.transpose(spread[:, q * P : (q + 1) * P], head_cols[:, q, :], ident[:])
+            nc.tensor.transpose(spread[:, q * P : (q + 1) * P], wgt_cols[:, q, :], ident[:])
         nc.scalar.copy(weights[:], spread[:])
-        b_ps = psum.tile([P, P], F32, name="b_ps", tag="acc7")
-        nc.tensor.transpose(b_ps[:], b_rows[:], ident[:])
-        nc.scalar.copy(b_cols[:], b_ps[:, 0:NB])
+        b_turned = psum.tile([P, P], F32, name="b_turned", tag="acc7")
+        nc.tensor.transpose(b_turned[:], b_rows[:], ident[:])
+        nc.scalar.copy(b_cols[:], b_turned[:, 0:BANDS])
 
-        c_bf = [keep.tile([P, HALF, PACK], BF16, name=f"c_bf{h}", align_bytes=64) for h in range(2)]
+        c_woven = [keep.tile([P, HALF, PACK], BF16, name=f"c_woven{h}", align_bytes=64) for h in range(2)]
         c_codes = keep.tile([P, S], U32, name="c_codes", align_bytes=64)
         c_scales = keep.tile([P, S], U8, name="c_scales", align_bytes=64)
-        g_early = keep.tile([P, 2, S], F32, name="g_early")
-        g_late = [keep.tile([P, 2, hi - lo], F32, name=f"g_late{lo}") for lo, hi in G_PARTS]
-        u_bf = [keep.tile([P, P, PACK], BF16, name=f"u_bf{n}", tag=f"u_bf{n}", align_bytes=64) for n in range(NB)]
+        picks_early = keep.tile([P, 2, S], F32, name="picks_early")
+        picks_late = [keep.tile([P, 2, HALF], F32, name=f"picks_late{h}") for h in range(2)]
+        u_woven = [
+            keep.tile([P, P, PACK], BF16, name=f"u_woven{n}", tag=f"u_woven{n}", align_bytes=64) for n in range(BANDS)
+        ]
         u_codes = keep.tile([P, M], U32, name="u_codes", align_bytes=64)
         u_scales = keep.tile([P, M], U8, name="u_scales", align_bytes=64)
-        xg_bf = [keep.tile([P, HALF, PACK], BF16, name=f"xg_bf{h}", align_bytes=64) for h in range(2)]
+        xg_woven = [keep.tile([P, HALF, PACK], BF16, name=f"xg_woven{h}", align_bytes=64) for h in range(2)]
         xg_codes = keep.tile([P, S], U32, name="xg_codes", align_bytes=64)
         xg_scales = keep.tile([P, S], U8, name="xg_scales", align_bytes=64)
 
-        def lay(engine, dst, src):
-            (nc.scalar.copy if engine == "S" else nc.vector.tensor_copy)(
-                dst.rearrange("p (r i) j -> p r j i", i=4), src.rearrange("p j (r i) -> p r j i", i=4)
-            )
+        def weave(copy, dst, src):
+            copy(dst.rearrange("p (r e) i -> p r i e", e=4), src.rearrange("p i (r e) -> p r i e", e=4))
 
-        def quant(codes, scales, src):
-            nc.vector.quantize_mx(out=codes.bitcast(E4M3X4), scales=scales, in_=src.rearrange("p w j -> p (w j)"))
+        def quantise(codes, scales, woven):
+            nc.vector.quantize_mx(out=codes.bitcast(E4M3X4), scales=scales, in_=woven.rearrange("p w i -> p (w i)"))
 
         for i in range(2):
-            nc.vector.tensor_tensor(g_early[:, i, :], planes[i][:].indirect(offsets[:]), weights[:], MULT)
-        halves = [slice(h * HALF, (h + 1) * HALF) for h in range(2)]
+            nc.vector.tensor_tensor(picks_early[:, i, :], planes[i][:].indirect(offsets[:]), weights[:], MULT)
         for h in range(2):
-            lay("S", xg_bf[h][:, :, 0:2], g_early[:, :, halves[h]])
+            weave(nc.scalar.copy, xg_woven[h][:, :, 0:2], picks_early[:, :, HALVES[h]])
         for i in range(2):
-            for h, (lo, hi) in enumerate(G_PARTS):
-                nc.vector.tensor_tensor(
-                    g_late[h][:, i, :], planes[2 + i][:].indirect(offsets[:, lo // 16 : hi // 16]), weights[:, lo:hi], MULT
-                )
-        for part, (lo, hi) in enumerate(G_PARTS):
-            h = lo // HALF
-            lay("V", xg_bf[h][:, lo - h * HALF : hi - h * HALF, 2:4], g_late[part][:])
+            for h, cols in enumerate(HALVES):
+                window = planes[2 + i][:].indirect(offsets[:, cols.start // GROUP : cols.stop // GROUP])
+                nc.vector.tensor_tensor(picks_late[h][:, i, :], window, weights[:, cols], MULT)
         for h in range(2):
-            quant(xg_codes[:, halves[h]], xg_scales[:, halves[h]], xg_bf[h][:])
-        for h in range(2):
-            lay("S", c_bf[h][:], c_raw[h][:])
-        for h in range(2):
-            quant(c_codes[:, halves[h]], c_scales[:, halves[h]], c_bf[h][:])
-        accs = [psum.tile([P, S], F32, name=f"acc{n}", tag=f"acc{n}") for n in range(NB)]
+            weave(nc.vector.tensor_copy, xg_woven[h][:, :, 2:4], picks_late[h][:])
+        for h, cols in enumerate(HALVES):
+            quantise(xg_codes[:, cols], xg_scales[:, cols], xg_woven[h][:])
 
-        def w_pass(n, start):
-            h = 0 if n < W_FIRST else 1
-            k = 2 * P * (n - h * W_FIRST)
+        for h in range(2):
+            weave(nc.scalar.copy, c_woven[h][:], c_raw[h][:])
+        for h, cols in enumerate(HALVES):
+            quantise(c_codes[:, cols], c_scales[:, cols], c_woven[h][:])
+
+        accs = [psum.tile([P, S], F32, name=f"acc{n}", tag=f"acc{n}") for n in range(BANDS)]
+
+        def open_bank(n):
+            words, first = (w4_early, 0) if n < EARLY else (w4_late, EARLY)
             nc.tensor.matmul_mx(
                 out=accs[n][:],
-                lhsT=w4_t[h][:, k : k + 2 * P].bitcast(E2M1X4),
-                lhsT_scale=w4_s[:, P * n : P * (n + 1)],
+                lhsT=words[:, 2 * P * (n - first) : 2 * P * (n - first + 1)].bitcast(E2M1X4),
+                lhsT_scale=w4_scale_rows[:, P * n : P * (n + 1)],
                 rhs=xg_codes[:].bitcast(E4M3X4),
                 rhs_scale=xg_scales[:],
-                start=start,
-                stop=not start,
+                start=True,
+                stop=False,
             )
 
-        def u_pass(n, start):
+        def close_bank(n):
             nc.tensor.matmul_mx(
                 out=accs[n][:],
                 lhsT=u_codes[:, P * n : P * (n + 1)].bitcast(E4M3X4),
                 lhsT_scale=u_scales[:, P * n : P * (n + 1)],
                 rhs=c_codes[:].bitcast(E4M3X4),
                 rhs_scale=c_scales[:],
-                start=start,
-                stop=not start,
+                start=False,
+                stop=True,
             )
 
-        def finish(n):
-            tag = {0: f"u_raw{U_CUTS[1]}", NB - 2: f"u_bf{NB - 1}"}.get(n, f"res{n}")
-            res = keep.tile([P, S], F32, name=f"res{n}", tag=tag, align_bytes=64)
-            if n != NB - 2:
-                nc.scalar.activation(res[:], accs[n][:], IDENTITY, bias=b_cols[:, n : n + 1])
+        reused = {0: "u_raw1", VECTOR_EMPTIES: f"u_woven{BANDS - 1}"}
+
+        def empty_and_store(n):
+            result = keep.tile([P, S], F32, name=f"result{n}", tag=reused.get(n, f"result{n}"), align_bytes=64)
+            if n == VECTOR_EMPTIES:
+                nc.vector.tensor_scalar(result[:], accs[n][:], b_cols[:, n : n + 1], None, ADD)
             else:
-                nc.vector.tensor_scalar(res[:], accs[n][:], b_cols[:, n : n + 1], None, ADD)
-            nc.sync.dma_start(out[n * P : (n + 1) * P, :], res[:])
+                nc.scalar.activation(result[:], accs[n][:], IDENTITY, bias=b_cols[:, n : n + 1])
+            nc.sync.dma_start(out[n * P : (n + 1) * P, :], result[:])
 
-        def lay_u(engine, n):
-            q = max(i for i, (lo, hi) in enumerate(U_PARTS) if lo <= n * P)
-            k = n * P - U_CUTS[q]
-            lay(engine, u_bf[n][:], u_raw[q][:, :, k : k + P])
-
-        def quant_u(n):
-            quant(u_codes[:, n * P : (n + 1) * P], u_scales[:, n * P : (n + 1) * P], u_bf[n][:])
-
-        def banks(first, last):
-            for n in range(first, last):
-                if n in U_OPENS:
-                    u_pass(n, True)
-                    w_pass(n, False)
-                else:
-                    if n >= W_FIRST:
-                        w_pass(n, True)
-                    u_pass(n, False)
-                finish(n)
-
-        for n in range(W_FIRST):
-            w_pass(n, True)
-        for lo, hi in U_PARTS:
-            for n in range(lo // P, hi // P):
-                lay_u("S" if n == 1 else "V", n)
-            for n in range(lo // P, hi // P):
-                quant_u(n)
-        banks(0, NB)
+        for n in range(EARLY):
+            open_bank(n)
+        for q, piece in enumerate(U_PIECES):
+            for place, n in enumerate(piece):
+                copy = nc.scalar.copy if n == SCALAR_WEAVES else nc.vector.tensor_copy
+                weave(copy, u_woven[n][:], u_raw[q][:, :, place * P : (place + 1) * P])
+            for n in piece:
+                quantise(u_codes[:, n * P : (n + 1) * P], u_scales[:, n * P : (n + 1) * P], u_woven[n][:])
+        for n in range(BANDS):
+            if n >= EARLY:
+                open_bank(n)
+            close_bank(n)
+            empty_and_store(n)

@@ -23,9 +23,9 @@ GROUP = P // HEADS
 BANDS = M // P
 HALF = S // 2
 HALVES = (slice(0, HALF), slice(HALF, S))
-U_PIECES = ((0,), (1, 2), (3, 4), (5, 6), (7,))
+U_PIECES = ((0, 1), (2, 3), (4, 5), (6, 7))
 EARLY = 3
-SCALAR_WEAVES = 1
+SCALAR_WEAVES = 2
 VECTOR_EMPTIES = BANDS - 2
 
 FLOPS = 2 * M * S * (K + L)
@@ -40,7 +40,7 @@ def tile_list_hmix_bias_kernel(tc, xT, w4_words, w4_scales, c, u, wgt, b, offs, 
         offsets = keep.tile([P, S // GROUP], U16, name="offsets")
         weights = keep.tile([P, S], F32, name="weights")
         planes = [keep.tile([P, T], F32, name=f"plane{i}") for i in range(PACK)]
-        c_raw = [keep.tile([P, PACK, HALF], F32, name=f"c_raw{h}") for h in range(2)]
+        c_raw = keep.tile([P, PACK, S], F32, name="c_raw")
         u_raw = [
             keep.tile([P, PACK, P * len(piece)], F32, name=f"u_raw{q}", tag=f"u_raw{q}", align_bytes=64)
             for q, piece in enumerate(U_PIECES)
@@ -74,12 +74,11 @@ def tile_list_hmix_bias_kernel(tc, xT, w4_words, w4_scales, c, u, wgt, b, offs, 
             )
         for i in range(1, PACK):
             nc.sync.dma_start(planes[i][:], xv[:, i, :])
-        nc.sync.dma_start(c_raw[0][:], cv[:, :, HALVES[0]])
+        nc.sync.dma_start(c_raw[:], cv)
         nc.sync.dma_start(w4_early[:], w4_words[0, :, 0 : 2 * P * EARLY])
-        nc.sync.dma_start(c_raw[1][:], cv[:, :, HALVES[1]])
         for q, piece in enumerate(U_PIECES):
             nc.sync.dma_start(u_raw[q][:], uv[:, :, P * piece[0] : P * (piece[-1] + 1)])
-            if EARLY in piece:
+            if EARLY + 1 in piece:
                 nc.sync.dma_start(w4_late[:], w4_words[0, :, 2 * P * EARLY : 2 * M])
 
         turned = psum.tile([P, P], F32, name="turned", tag="acc6")
@@ -129,8 +128,8 @@ def tile_list_hmix_bias_kernel(tc, xT, w4_words, w4_scales, c, u, wgt, b, offs, 
         for h, cols in enumerate(HALVES):
             quantise(xg_codes[:, cols], xg_scales[:, cols], xg_woven[h][:])
 
-        for h in range(2):
-            weave(nc.scalar.copy, c_woven[h][:], c_raw[h][:])
+        for h, copy in enumerate((nc.scalar.copy, nc.vector.tensor_copy)):
+            weave(copy, c_woven[h][:], c_raw[:, :, HALVES[h]])
         for h, cols in enumerate(HALVES):
             quantise(c_codes[:, cols], c_scales[:, cols], c_woven[h][:])
 
@@ -159,7 +158,7 @@ def tile_list_hmix_bias_kernel(tc, xT, w4_words, w4_scales, c, u, wgt, b, offs, 
                 stop=True,
             )
 
-        reused = {0: "u_raw1", VECTOR_EMPTIES: f"u_woven{BANDS - 1}"}
+        reused = {0: "u_raw0", VECTOR_EMPTIES: f"u_woven{BANDS - 1}"}
 
         def empty_and_store(n):
             result = keep.tile([P, S], F32, name=f"result{n}", tag=reused.get(n, f"result{n}"), align_bytes=64)
@@ -173,7 +172,7 @@ def tile_list_hmix_bias_kernel(tc, xT, w4_words, w4_scales, c, u, wgt, b, offs, 
             open_bank(n)
         for q, piece in enumerate(U_PIECES):
             for place, n in enumerate(piece):
-                copy = nc.scalar.copy if n == SCALAR_WEAVES else nc.vector.tensor_copy
+                copy = nc.scalar.copy if n < SCALAR_WEAVES else nc.vector.tensor_copy
                 weave(copy, u_woven[n][:], u_raw[q][:, :, place * P : (place + 1) * P])
             for n in piece:
                 quantise(u_codes[:, n * P : (n + 1) * P], u_scales[:, n * P : (n + 1) * P], u_woven[n][:])

@@ -51,7 +51,6 @@ def tile_list_hmix_bias_kernel(tc, xT, w4_words, w4_scales, c, u, wgt, b, offs, 
         wgt_rows = keep.tile([P, P], F32, name="wgt_rows")
         b_rows = keep.tile([P, P], F32, name="b_rows")
         wgt_cols = keep.tile([P, S // P, P], F32, name="wgt_cols")
-        b_cols = keep.tile([P, BANDS], F32, name="b_cols")
         ident = keep.tile([P, P], F32, name="ident")
 
         xv = xT.rearrange("(p i) t -> p i t", i=PACK)
@@ -67,15 +66,15 @@ def tile_list_hmix_bias_kernel(tc, xT, w4_words, w4_scales, c, u, wgt, b, offs, 
         nc.sync.dma_start(wgt_rows[0:32, :], wgt.rearrange("(g r) (q m) -> g q r m", r=GROUP, m=P)[:, :, 0, :])
         nc.sync.dma_start(planes[0][:], xv[:, 0, :])
         nc.sync.dma_start(offsets[:], offs)
-        nc.scalar.dma_start(b_rows[0:BANDS, :], b.rearrange("(t m) -> t m", m=P))
-        for q in range(4):
-            nc.scalar.dma_start(
-                w4_scale_rows[32 * q : 32 * q + 4, :].bitcast(I32), w4_scales[0, 4 * q : 4 * q + 4, :].bitcast(I32)
-            )
         for i in range(1, PACK):
             nc.sync.dma_start(planes[i][:], xv[:, i, :])
-        nc.sync.dma_start(c_raw[:], cv)
+        nc.sync.dma_start(b_rows[0:BANDS, :], b.rearrange("(t m) -> t m", m=P))
         nc.sync.dma_start(w4_early[:], w4_words[0, :, 0 : 2 * P * EARLY])
+        nc.sync.dma_start(c_raw[:], cv)
+        for q in range(4):
+            nc.sync.dma_start(
+                w4_scale_rows[32 * q : 32 * q + 4, :].bitcast(I32), w4_scales[0, 4 * q : 4 * q + 4, :].bitcast(I32)
+            )
         for q, piece in enumerate(U_PIECES):
             nc.sync.dma_start(u_raw[q][:], uv[:, :, P * piece[0] : P * (piece[-1] + 1)])
             if EARLY + 1 in piece:
@@ -91,14 +90,11 @@ def tile_list_hmix_bias_kernel(tc, xT, w4_words, w4_scales, c, u, wgt, b, offs, 
         for q in range(S // P):
             nc.tensor.transpose(spread[:, q * P : (q + 1) * P], wgt_cols[:, q, :], ident[:])
         nc.scalar.copy(weights[:], spread[:])
-        b_turned = psum.tile([P, P], F32, name="b_turned", tag="acc7")
-        nc.tensor.transpose(b_turned[:], b_rows[:], ident[:])
-        nc.scalar.copy(b_cols[:], b_turned[:, 0:BANDS])
 
         c_woven = [keep.tile([P, HALF, PACK], BF16, name=f"c_woven{h}", align_bytes=64) for h in range(2)]
         c_codes = keep.tile([P, S], U32, name="c_codes", align_bytes=64)
         c_scales = keep.tile([P, S], U8, name="c_scales", align_bytes=64)
-        picks_early = keep.tile([P, 2, S], F32, name="picks_early")
+        picks_early = keep.tile([P, 2, S], F32, name="picks_early", tag="picks_early")
         picks_late = [keep.tile([P, 2, HALF], F32, name=f"picks_late{h}") for h in range(2)]
         u_woven = [
             keep.tile([P, P, PACK], BF16, name=f"u_woven{n}", tag=f"u_woven{n}", align_bytes=64) for n in range(BANDS)
@@ -119,6 +115,10 @@ def tile_list_hmix_bias_kernel(tc, xT, w4_words, w4_scales, c, u, wgt, b, offs, 
             nc.vector.tensor_tensor(picks_early[:, i, :], planes[i][:].indirect(offsets[:]), weights[:], MULT)
         for h in range(2):
             weave(nc.scalar.copy, xg_woven[h][:, :, 0:2], picks_early[:, :, HALVES[h]])
+        b_cols = keep.tile([P, BANDS], F32, name="b_cols", tag="picks_early")
+        b_turned = psum.tile([P, P], F32, name="b_turned", tag="acc7")
+        nc.tensor.transpose(b_turned[:], b_rows[:], ident[:])
+        nc.scalar.copy(b_cols[:], b_turned[:, 0:BANDS])
         for i in range(2):
             for h, cols in enumerate(HALVES):
                 window = planes[2 + i][:].indirect(offsets[:, cols.start // GROUP : cols.stop // GROUP])

@@ -28,6 +28,8 @@ EARLY = 3
 SCALAR_WEAVES = 2
 VECTOR_EMPTIES = BANDS - 2
 
+C_SCALAR = 288
+
 FLOPS = 2 * M * S * (K + L)
 
 
@@ -66,11 +68,11 @@ def tile_list_hmix_bias_kernel(tc, xT, w4_words, w4_scales, c, u, wgt, b, offs, 
         nc.sync.dma_start(wgt_rows[0:32, :], wgt.rearrange("(g r) (q m) -> g q r m", r=GROUP, m=P)[:, :, 0, :])
         nc.sync.dma_start(planes[0][:], xv[:, 0, :])
         nc.sync.dma_start(offsets[:], offs)
+        nc.sync.dma_start(b_rows[0:BANDS, :], b.rearrange("(t m) -> t m", m=P))
         for i in range(1, PACK):
             nc.sync.dma_start(planes[i][:], xv[:, i, :])
-        nc.sync.dma_start(b_rows[0:BANDS, :], b.rearrange("(t m) -> t m", m=P))
-        nc.sync.dma_start(w4_early[:], w4_words[0, :, 0 : 2 * P * EARLY])
         nc.sync.dma_start(c_raw[:], cv)
+        nc.sync.dma_start(w4_early[:], w4_words[0, :, 0 : 2 * P * EARLY])
         for q in range(4):
             nc.sync.dma_start(
                 w4_scale_rows[32 * q : 32 * q + 4, :].bitcast(I32), w4_scales[0, 4 * q : 4 * q + 4, :].bitcast(I32)
@@ -91,7 +93,7 @@ def tile_list_hmix_bias_kernel(tc, xT, w4_words, w4_scales, c, u, wgt, b, offs, 
             nc.tensor.transpose(spread[:, q * P : (q + 1) * P], wgt_cols[:, q, :], ident[:])
         nc.scalar.copy(weights[:], spread[:])
 
-        c_woven = [keep.tile([P, HALF, PACK], BF16, name=f"c_woven{h}", align_bytes=64) for h in range(2)]
+        c_woven = keep.tile([P, S, PACK], BF16, name="c_woven", align_bytes=64)
         c_codes = keep.tile([P, S], U32, name="c_codes", align_bytes=64)
         c_scales = keep.tile([P, S], U8, name="c_scales", align_bytes=64)
         picks_early = keep.tile([P, 2, S], F32, name="picks_early", tag="picks_early")
@@ -123,15 +125,15 @@ def tile_list_hmix_bias_kernel(tc, xT, w4_words, w4_scales, c, u, wgt, b, offs, 
             for h, cols in enumerate(HALVES):
                 window = planes[2 + i][:].indirect(offsets[:, cols.start // GROUP : cols.stop // GROUP])
                 nc.vector.tensor_tensor(picks_late[h][:, i, :], window, weights[:, cols], MULT)
-        for h in range(2):
-            weave(nc.vector.tensor_copy, xg_woven[h][:, :, 2:4], picks_late[h][:])
+        for h, copy in enumerate((nc.scalar.copy, nc.vector.tensor_copy)):
+            weave(copy, xg_woven[h][:, :, 2:4], picks_late[h][:])
         for h, cols in enumerate(HALVES):
             quantise(xg_codes[:, cols], xg_scales[:, cols], xg_woven[h][:])
 
-        for h, copy in enumerate((nc.scalar.copy, nc.vector.tensor_copy)):
-            weave(copy, c_woven[h][:], c_raw[:, :, HALVES[h]])
+        weave(nc.scalar.copy, c_woven[:, 0:C_SCALAR, :], c_raw[:, :, 0:C_SCALAR])
+        weave(nc.vector.tensor_copy, c_woven[:, C_SCALAR:S, :], c_raw[:, :, C_SCALAR:S])
         for h, cols in enumerate(HALVES):
-            quantise(c_codes[:, cols], c_scales[:, cols], c_woven[h][:])
+            quantise(c_codes[:, cols], c_scales[:, cols], c_woven[:, cols, :])
 
         accs = [psum.tile([P, S], F32, name=f"acc{n}", tag=f"acc{n}") for n in range(BANDS)]
 
@@ -170,12 +172,24 @@ def tile_list_hmix_bias_kernel(tc, xT, w4_words, w4_scales, c, u, wgt, b, offs, 
 
         for n in range(EARLY):
             open_bank(n)
-        for q, piece in enumerate(U_PIECES):
-            for place, n in enumerate(piece):
-                copy = nc.scalar.copy if n < SCALAR_WEAVES else nc.vector.tensor_copy
-                weave(copy, u_woven[n][:], u_raw[q][:, :, place * P : (place + 1) * P])
-            for n in piece:
-                quantise(u_codes[:, n * P : (n + 1) * P], u_scales[:, n * P : (n + 1) * P], u_woven[n][:])
+        def weave_u(copy, n, lo, hi):
+            q, place = divmod(n, 2)
+            weave(copy, u_woven[n][:, lo:hi, :], u_raw[q][:, :, place * P + lo : place * P + hi])
+
+        def quantise_u(n):
+            cols = slice(n * P, (n + 1) * P)
+            quantise(u_codes[:, cols], u_scales[:, cols], u_woven[n][:])
+
+        weave_u(nc.scalar.copy, 0, 0, P)
+        weave_u(nc.scalar.copy, 1, 0, P // 2)
+        weave_u(nc.vector.tensor_copy, 1, P // 2, P)
+        quantise_u(0)
+        quantise_u(1)
+        for n in range(2, BANDS, 2):
+            weave_u(nc.vector.tensor_copy, n, 0, P)
+            weave_u(nc.vector.tensor_copy, n + 1, 0, P)
+            quantise_u(n)
+            quantise_u(n + 1)
         for n in range(BANDS):
             if n >= EARLY:
                 open_bank(n)

@@ -23,7 +23,7 @@ GROUP = P // HEADS
 BANDS = M // P
 HALF = S // 2
 HALVES = (slice(0, HALF), slice(HALF, S))
-U_PIECES = ((0, 1), (2, 3), (4, 5), (6, 7))
+U_PIECES = ((0, 1), (2, 3), (4, 5), (6,), (7,))
 EARLY = 3
 SCALAR_WEAVES = 2
 VECTOR_EMPTIES = BANDS - 2
@@ -137,15 +137,15 @@ def tile_list_hmix_bias_kernel(tc, xT, w4_words, w4_scales, c, u, wgt, b, offs, 
 
         accs = [psum.tile([P, S], F32, name=f"acc{n}", tag=f"acc{n}") for n in range(BANDS)]
 
-        def open_bank(n):
+        def open_bank(n, cols=slice(0, S)):
             words, first = (w4_early, 0) if n < EARLY else (w4_late, EARLY)
             nc.tensor.matmul_mx(
-                out=accs[n][:],
+                out=accs[n][:, cols],
                 lhsT=words[:, 2 * P * (n - first) : 2 * P * (n - first + 1)].bitcast(E2M1X4),
                 lhsT_scale=w4_scale_rows[:, P * n : P * (n + 1)],
-                rhs=xg_codes[:].bitcast(E4M3X4),
-                rhs_scale=xg_scales[:],
-                start=True,
+                rhs=xg_codes[:, cols].bitcast(E4M3X4),
+                rhs_scale=xg_scales[:, cols],
+                start=cols.start == 0,
                 stop=False,
             )
 
@@ -170,10 +170,12 @@ def tile_list_hmix_bias_kernel(tc, xT, w4_words, w4_scales, c, u, wgt, b, offs, 
                 nc.scalar.activation(result[:], accs[n][:], IDENTITY, bias=b_cols[:, n : n + 1])
             nc.sync.dma_start(out[n * P : (n + 1) * P, :], result[:])
 
-        for n in range(EARLY):
-            open_bank(n)
+        for half in HALVES:
+            for n in range(EARLY):
+                for lo in range(half.start, half.stop, P):
+                    open_bank(n, slice(lo, lo + P))
         def weave_u(copy, n, lo, hi):
-            q, place = divmod(n, 2)
+            q, place = [(q, piece.index(n)) for q, piece in enumerate(U_PIECES) if n in piece][0]
             weave(copy, u_woven[n][:, lo:hi, :], u_raw[q][:, :, place * P + lo : place * P + hi])
 
         def quantise_u(n):

@@ -28,7 +28,8 @@ EARLY = 3
 SCALAR_WEAVES = 2
 VECTOR_EMPTIES = BANDS - 2
 
-C_SCALAR = 288
+C_SCALAR = 272
+SHARED = BANDS - 2
 
 FLOPS = 2 * M * S * (K + L)
 
@@ -93,7 +94,6 @@ def tile_list_hmix_bias_kernel(tc, xT, w4_words, w4_scales, c, u, wgt, b, offs, 
             nc.tensor.transpose(spread[:, q * P : (q + 1) * P], wgt_cols[:, q, :], ident[:])
         nc.scalar.copy(weights[:], spread[:])
 
-        c_woven = keep.tile([P, S, PACK], BF16, name="c_woven", align_bytes=64)
         c_codes = keep.tile([P, S], U32, name="c_codes", align_bytes=64)
         c_scales = keep.tile([P, S], U8, name="c_scales", align_bytes=64)
         picks_early = keep.tile([P, 2, S], F32, name="picks_early", tag="picks_early")
@@ -103,7 +103,7 @@ def tile_list_hmix_bias_kernel(tc, xT, w4_words, w4_scales, c, u, wgt, b, offs, 
         ]
         u_codes = keep.tile([P, M], U32, name="u_codes", align_bytes=64)
         u_scales = keep.tile([P, M], U8, name="u_scales", align_bytes=64)
-        xg_woven = [keep.tile([P, HALF, PACK], BF16, name=f"xg_woven{h}", align_bytes=64) for h in range(2)]
+        xg_woven = [keep.tile([P, HALF, PACK], BF16, name=f"xg_woven{h}", tag=f"xg_woven{h}", align_bytes=64) for h in range(2)]
         xg_codes = keep.tile([P, S], U32, name="xg_codes", align_bytes=64)
         xg_scales = keep.tile([P, S], U8, name="xg_scales", align_bytes=64)
 
@@ -125,37 +125,43 @@ def tile_list_hmix_bias_kernel(tc, xT, w4_words, w4_scales, c, u, wgt, b, offs, 
             for h, cols in enumerate(HALVES):
                 window = planes[2 + i][:].indirect(offsets[:, cols.start // GROUP : cols.stop // GROUP])
                 nc.vector.tensor_tensor(picks_late[h][:, i, :], window, weights[:, cols], MULT)
-        for h, copy in enumerate((nc.scalar.copy, nc.vector.tensor_copy)):
-            weave(copy, xg_woven[h][:, :, 2:4], picks_late[h][:])
+        weave(nc.scalar.copy, xg_woven[0][:, :, 2:4], picks_late[0][:])
+        weave(nc.scalar.copy, xg_woven[1][:, 0:P, 2:4], picks_late[1][:, :, 0:P])
+        weave(nc.vector.tensor_copy, xg_woven[1][:, P:HALF, 2:4], picks_late[1][:, :, P:HALF])
         for h, cols in enumerate(HALVES):
             quantise(xg_codes[:, cols], xg_scales[:, cols], xg_woven[h][:])
 
-        weave(nc.scalar.copy, c_woven[:, 0:C_SCALAR, :], c_raw[:, :, 0:C_SCALAR])
-        weave(nc.vector.tensor_copy, c_woven[:, C_SCALAR:S, :], c_raw[:, :, C_SCALAR:S])
+        c_woven = [
+            keep.tile([P, HALF, PACK], BF16, name=f"c_woven{h}", tag=tag, align_bytes=64)
+            for h, tag in enumerate(("c_woven0", "xg_woven1"))
+        ]
+        weave(nc.scalar.copy, c_woven[0][:], c_raw[:, :, 0:HALF])
+        weave(nc.scalar.copy, c_woven[1][:, 0 : C_SCALAR - HALF, :], c_raw[:, :, HALF:C_SCALAR])
+        weave(nc.vector.tensor_copy, c_woven[1][:, C_SCALAR - HALF : HALF, :], c_raw[:, :, C_SCALAR:S])
         for h, cols in enumerate(HALVES):
-            quantise(c_codes[:, cols], c_scales[:, cols], c_woven[:, cols, :])
+            quantise(c_codes[:, cols], c_scales[:, cols], c_woven[h][:])
 
-        accs = [psum.tile([P, S], F32, name=f"acc{n}", tag=f"acc{n}") for n in range(BANDS)]
+        accs = {n: psum.tile([P, S], F32, name=f"acc{n}", tag=f"acc{n}") for n in range(SHARED)}
 
-        def open_bank(n, cols=slice(0, S)):
+        def open_bank(n, cols, acc, start):
             words, first = (w4_early, 0) if n < EARLY else (w4_late, EARLY)
             nc.tensor.matmul_mx(
-                out=accs[n][:, cols],
+                out=acc,
                 lhsT=words[:, 2 * P * (n - first) : 2 * P * (n - first + 1)].bitcast(E2M1X4),
                 lhsT_scale=w4_scale_rows[:, P * n : P * (n + 1)],
                 rhs=xg_codes[:, cols].bitcast(E4M3X4),
                 rhs_scale=xg_scales[:, cols],
-                start=cols.start == 0,
+                start=start,
                 stop=False,
             )
 
-        def close_bank(n):
+        def close_bank(n, cols, acc):
             nc.tensor.matmul_mx(
-                out=accs[n][:],
+                out=acc,
                 lhsT=u_codes[:, P * n : P * (n + 1)].bitcast(E4M3X4),
                 lhsT_scale=u_scales[:, P * n : P * (n + 1)],
-                rhs=c_codes[:].bitcast(E4M3X4),
-                rhs_scale=c_scales[:],
+                rhs=c_codes[:, cols].bitcast(E4M3X4),
+                rhs_scale=c_scales[:, cols],
                 start=False,
                 stop=True,
             )
@@ -164,8 +170,9 @@ def tile_list_hmix_bias_kernel(tc, xT, w4_words, w4_scales, c, u, wgt, b, offs, 
 
         def empty_and_store(n):
             result = keep.tile([P, S], F32, name=f"result{n}", tag=reused.get(n, f"result{n}"), align_bytes=64)
-            if n == VECTOR_EMPTIES:
-                nc.vector.tensor_scalar(result[:], accs[n][:], b_cols[:, n : n + 1], None, ADD)
+            if n >= SHARED:
+                nc.vector.tensor_scalar(result[:, HALVES[0]], accs[n, 0][:], b_cols[:, n : n + 1], None, ADD)
+                nc.scalar.activation(result[:, HALVES[1]], accs[n, 1][:], IDENTITY, bias=b_cols[:, n : n + 1])
             else:
                 nc.scalar.activation(result[:], accs[n][:], IDENTITY, bias=b_cols[:, n : n + 1])
             nc.sync.dma_start(out[n * P : (n + 1) * P, :], result[:])
@@ -173,7 +180,7 @@ def tile_list_hmix_bias_kernel(tc, xT, w4_words, w4_scales, c, u, wgt, b, offs, 
         for half in HALVES:
             for n in range(EARLY):
                 for lo in range(half.start, half.stop, P):
-                    open_bank(n, slice(lo, lo + P))
+                    open_bank(n, slice(lo, lo + P), accs[n][:, lo : lo + P], lo == 0)
         def weave_u(copy, n, lo, hi):
             q, place = [(q, piece.index(n)) for q, piece in enumerate(U_PIECES) if n in piece][0]
             weave(copy, u_woven[n][:, lo:hi, :], u_raw[q][:, :, place * P + lo : place * P + hi])
@@ -193,7 +200,15 @@ def tile_list_hmix_bias_kernel(tc, xT, w4_words, w4_scales, c, u, wgt, b, offs, 
             quantise_u(n)
             quantise_u(n + 1)
         for n in range(BANDS):
-            if n >= EARLY:
-                open_bank(n)
-            close_bank(n)
+            if n >= SHARED:
+                for h, cols in enumerate(HALVES):
+                    bank = n if h == 0 else n - SHARED
+                    accs[n, h] = psum.tile([P, HALF], F32, name=f"acc{n}_{h}", tag=f"acc{bank}")
+                    open_bank(n, cols, accs[n, h][:], True)
+                for h, cols in enumerate(HALVES):
+                    close_bank(n, cols, accs[n, h][:])
+            else:
+                if n >= EARLY:
+                    open_bank(n, slice(0, S), accs[n][:], True)
+                close_bank(n, slice(0, S), accs[n][:])
             empty_and_store(n)

@@ -17,17 +17,16 @@ IDENTITY = mybir.ActivationFunctionType.Identity
 
 P = 128
 PACK = 4
+QUADRANT = 32
 K, L, M, T, S = 512, 512, 1024, 2048, 512
 HEADS = 8
 GROUP = P // HEADS
+RUNS = S // P
 BANDS = M // P
 HALF = S // 2
 HALVES = (slice(0, HALF), slice(HALF, S))
 U_PIECES = ((0, 1), (2, 3), (4, 5), (6,), (7,))
 EARLY = 3
-SCALAR_WEAVES = 2
-VECTOR_EMPTIES = BANDS - 2
-
 C_SCALAR = 272
 SHARED = BANDS - 2
 
@@ -53,44 +52,48 @@ def tile_list_hmix_bias_kernel(tc, xT, w4_words, w4_scales, c, u, wgt, b, offs, 
         w4_scale_rows = keep.tile([P, M], U8, name="w4_scale_rows", align_bytes=64)
         wgt_rows = keep.tile([P, P], F32, name="wgt_rows")
         b_rows = keep.tile([P, P], F32, name="b_rows")
-        wgt_cols = keep.tile([P, S // P, P], F32, name="wgt_cols")
+        wgt_cols = keep.tile([P, RUNS, P], F32, name="wgt_cols")
         ident = keep.tile([P, P], F32, name="ident")
 
         xv = xT.rearrange("(p i) t -> p i t", i=PACK)
         cv = c.rearrange("(p i) s -> p i s", i=PACK)
         uv = u.rearrange("(p i) n -> p i n", i=PACK)
 
-        nc.gpsimd.memset(w4_scale_rows[:].bitcast(I32), 0)
         nc.gpsimd.memset(b_rows[:], 0.0)
-        nc.vector.memset(wgt_rows[32:64, :], 0.0)
-        nc.vector.memset(wgt_rows[64:P, :], 0.0)
+        nc.gpsimd.memset(w4_scale_rows[:].bitcast(I32), 0)
+        nc.vector.memset(wgt_rows[QUADRANT : 2 * QUADRANT, :], 0.0)
+        nc.vector.memset(wgt_rows[2 * QUADRANT : P, :], 0.0)
         make_identity(nc, ident[:])
 
-        nc.sync.dma_start(wgt_rows[0:32, :], wgt.rearrange("(g r) (q m) -> g q r m", r=GROUP, m=P)[:, :, 0, :])
-        nc.sync.dma_start(planes[0][:], xv[:, 0, :])
+        wgt_runs = wgt.rearrange("(g r) (q m) -> g q r m", r=GROUP, m=P)[:, :, 0, :]
+        nc.scalar.dma_start(wgt_rows[0 : HEADS * RUNS, :], wgt_runs)
+        nc.scalar.dma_start(b_rows[0:BANDS, :], b.rearrange("(t m) -> t m", m=P))
         nc.sync.dma_start(offsets[:], offs)
-        nc.sync.dma_start(b_rows[0:BANDS, :], b.rearrange("(t m) -> t m", m=P))
-        for i in range(1, PACK):
+        for i in range(PACK):
             nc.sync.dma_start(planes[i][:], xv[:, i, :])
         nc.sync.dma_start(c_raw[:], cv)
         nc.sync.dma_start(w4_early[:], w4_words[0, :, 0 : 2 * P * EARLY])
-        for q in range(4):
+        for q in range(P // QUADRANT):
             nc.sync.dma_start(
-                w4_scale_rows[32 * q : 32 * q + 4, :].bitcast(I32), w4_scales[0, 4 * q : 4 * q + 4, :].bitcast(I32)
+                w4_scale_rows[QUADRANT * q : QUADRANT * q + 4, :].bitcast(I32),
+                w4_scales[0, 4 * q : 4 * q + 4, :].bitcast(I32),
             )
         for q, piece in enumerate(U_PIECES):
             nc.sync.dma_start(u_raw[q][:], uv[:, :, P * piece[0] : P * (piece[-1] + 1)])
             if EARLY + 1 in piece:
                 nc.sync.dma_start(w4_late[:], w4_words[0, :, 2 * P * EARLY : 2 * M])
 
-        turned = psum.tile([P, P], F32, name="turned", tag="acc6")
+        turned = psum.tile([P, P], F32, name="turned", tag="bank6")
         nc.tensor.transpose(turned[:], wgt_rows[:], ident[:])
         nc.vector.tensor_copy(
             wgt_cols[:].rearrange("m q (g r) -> m q g r", g=HEADS),
-            turned[:, 0:32].rearrange("m (g q) -> m q g", g=HEADS).unsqueeze(3).to_broadcast([P, S // P, HEADS, GROUP]),
+            turned[:, 0 : HEADS * RUNS]
+            .rearrange("m (g q) -> m q g", g=HEADS)
+            .unsqueeze(3)
+            .to_broadcast([P, RUNS, HEADS, GROUP]),
         )
-        spread = psum.tile([P, S], F32, name="spread", tag="acc5")
-        for q in range(S // P):
+        spread = psum.tile([P, S], F32, name="spread", tag="bank5")
+        for q in range(RUNS):
             nc.tensor.transpose(spread[:, q * P : (q + 1) * P], wgt_cols[:, q, :], ident[:])
         nc.scalar.copy(weights[:], spread[:])
 
@@ -103,7 +106,9 @@ def tile_list_hmix_bias_kernel(tc, xT, w4_words, w4_scales, c, u, wgt, b, offs, 
         ]
         u_codes = keep.tile([P, M], U32, name="u_codes", align_bytes=64)
         u_scales = keep.tile([P, M], U8, name="u_scales", align_bytes=64)
-        xg_woven = [keep.tile([P, HALF, PACK], BF16, name=f"xg_woven{h}", tag=f"xg_woven{h}", align_bytes=64) for h in range(2)]
+        xg_woven = [
+            keep.tile([P, HALF, PACK], BF16, name=f"xg_woven{h}", tag=f"xg_woven{h}", align_bytes=64) for h in range(2)
+        ]
         xg_codes = keep.tile([P, S], U32, name="xg_codes", align_bytes=64)
         xg_scales = keep.tile([P, S], U8, name="xg_scales", align_bytes=64)
 
@@ -115,10 +120,10 @@ def tile_list_hmix_bias_kernel(tc, xT, w4_words, w4_scales, c, u, wgt, b, offs, 
 
         for i in range(2):
             nc.vector.tensor_tensor(picks_early[:, i, :], planes[i][:].indirect(offsets[:]), weights[:], MULT)
-        for h in range(2):
-            weave(nc.scalar.copy, xg_woven[h][:, :, 0:2], picks_early[:, :, HALVES[h]])
+        for h, cols in enumerate(HALVES):
+            weave(nc.scalar.copy, xg_woven[h][:, :, 0:2], picks_early[:, :, cols])
         b_cols = keep.tile([P, BANDS], F32, name="b_cols", tag="picks_early")
-        b_turned = psum.tile([P, P], F32, name="b_turned", tag="acc7")
+        b_turned = psum.tile([P, P], F32, name="b_turned", tag="bank7")
         nc.tensor.transpose(b_turned[:], b_rows[:], ident[:])
         nc.scalar.copy(b_cols[:], b_turned[:, 0:BANDS])
         for i in range(2):
@@ -141,9 +146,7 @@ def tile_list_hmix_bias_kernel(tc, xT, w4_words, w4_scales, c, u, wgt, b, offs, 
         for h, cols in enumerate(HALVES):
             quantise(c_codes[:, cols], c_scales[:, cols], c_woven[h][:])
 
-        accs = {n: psum.tile([P, S], F32, name=f"acc{n}", tag=f"acc{n}") for n in range(SHARED)}
-
-        def open_bank(n, cols, acc, start):
+        def w4_pass(n, cols, acc, start):
             words, first = (w4_early, 0) if n < EARLY else (w4_late, EARLY)
             nc.tensor.matmul_mx(
                 out=acc,
@@ -155,7 +158,7 @@ def tile_list_hmix_bias_kernel(tc, xT, w4_words, w4_scales, c, u, wgt, b, offs, 
                 stop=False,
             )
 
-        def close_bank(n, cols, acc):
+        def u_pass(n, cols, acc):
             nc.tensor.matmul_mx(
                 out=acc,
                 lhsT=u_codes[:, P * n : P * (n + 1)].bitcast(E4M3X4),
@@ -166,28 +169,19 @@ def tile_list_hmix_bias_kernel(tc, xT, w4_words, w4_scales, c, u, wgt, b, offs, 
                 stop=True,
             )
 
-        reused = {0: "u_raw0", VECTOR_EMPTIES: f"u_woven{BANDS - 1}"}
-
-        def empty_and_store(n):
-            result = keep.tile([P, S], F32, name=f"result{n}", tag=reused.get(n, f"result{n}"), align_bytes=64)
-            if n >= SHARED:
-                nc.vector.tensor_scalar(result[:, HALVES[0]], accs[n, 0][:], b_cols[:, n : n + 1], None, ADD)
-                nc.scalar.activation(result[:, HALVES[1]], accs[n, 1][:], IDENTITY, bias=b_cols[:, n : n + 1])
-            else:
-                nc.scalar.activation(result[:], accs[n][:], IDENTITY, bias=b_cols[:, n : n + 1])
-            nc.sync.dma_start(out[n * P : (n + 1) * P, :], result[:])
-
-        for half in HALVES:
-            for n in range(EARLY):
-                for lo in range(half.start, half.stop, P):
-                    open_bank(n, slice(lo, lo + P), accs[n][:, lo : lo + P], lo == 0)
         def weave_u(copy, n, lo, hi):
             q, place = [(q, piece.index(n)) for q, piece in enumerate(U_PIECES) if n in piece][0]
             weave(copy, u_woven[n][:, lo:hi, :], u_raw[q][:, :, place * P + lo : place * P + hi])
 
         def quantise_u(n):
-            cols = slice(n * P, (n + 1) * P)
-            quantise(u_codes[:, cols], u_scales[:, cols], u_woven[n][:])
+            rows = slice(n * P, (n + 1) * P)
+            quantise(u_codes[:, rows], u_scales[:, rows], u_woven[n][:])
+
+        accs = [psum.tile([P, S], F32, name=f"acc{n}", tag=f"bank{n}") for n in range(SHARED)]
+        for half in HALVES:
+            for n in range(EARLY):
+                for lo in range(half.start, half.stop, P):
+                    w4_pass(n, slice(lo, lo + P), accs[n][:, lo : lo + P], lo == 0)
 
         weave_u(nc.scalar.copy, 0, 0, P)
         weave_u(nc.scalar.copy, 1, 0, P // 2)
@@ -199,16 +193,25 @@ def tile_list_hmix_bias_kernel(tc, xT, w4_words, w4_scales, c, u, wgt, b, offs, 
             weave_u(nc.vector.tensor_copy, n + 1, 0, P)
             quantise_u(n)
             quantise_u(n + 1)
+
+        reused = {0: "u_raw0", SHARED: f"u_woven{BANDS - 1}"}
         for n in range(BANDS):
-            if n >= SHARED:
-                for h, cols in enumerate(HALVES):
-                    bank = n if h == 0 else n - SHARED
-                    accs[n, h] = psum.tile([P, HALF], F32, name=f"acc{n}_{h}", tag=f"acc{bank}")
-                    open_bank(n, cols, accs[n, h][:], True)
-                for h, cols in enumerate(HALVES):
-                    close_bank(n, cols, accs[n, h][:])
-            else:
+            bias = b_cols[:, n : n + 1]
+            if n < SHARED:
                 if n >= EARLY:
-                    open_bank(n, slice(0, S), accs[n][:], True)
-                close_bank(n, slice(0, S), accs[n][:])
-            empty_and_store(n)
+                    w4_pass(n, slice(0, S), accs[n][:], True)
+                u_pass(n, slice(0, S), accs[n][:])
+            else:
+                halves = []
+                for cols, bank in zip(HALVES, (n, n - SHARED)):
+                    halves.append(psum.tile([P, HALF], F32, name=f"acc{n}_{cols.start}", tag=f"bank{bank}"))
+                    w4_pass(n, cols, halves[-1][:], True)
+                for cols, acc in zip(HALVES, halves):
+                    u_pass(n, cols, acc[:])
+            result = keep.tile([P, S], F32, name=f"result{n}", tag=reused.get(n, f"result{n}"), align_bytes=64)
+            if n < SHARED:
+                nc.scalar.activation(result[:], accs[n][:], IDENTITY, bias=bias)
+            else:
+                nc.vector.tensor_scalar(result[:, HALVES[0]], halves[0][:], bias, None, ADD)
+                nc.scalar.activation(result[:, HALVES[1]], halves[1][:], IDENTITY, bias=bias)
+            nc.sync.dma_start(out[n * P : (n + 1) * P, :], result[:])

@@ -25,8 +25,9 @@ RUNS = S // P
 BANDS = M // P
 HALF = S // 2
 HALVES = (slice(0, HALF), slice(HALF, S))
-U_PIECES = ((0, 1), (2, 3), (4, 5), (6,), (7,))
+U_PIECES = ((0, 1), (2, 3), (4, 5), (6, 7))
 EARLY = 3
+W4_SPANS = ((0, EARLY), (EARLY, BANDS - 2), (BANDS - 2, BANDS))
 C_SCALAR = 272
 SHARED = BANDS - 2
 
@@ -47,8 +48,9 @@ def tile_list_hmix_bias_kernel(tc, xT, w4_words, w4_scales, c, u, wgt, b, offs, 
             keep.tile([P, PACK, P * len(piece)], F32, name=f"u_raw{q}", tag=f"u_raw{q}", align_bytes=64)
             for q, piece in enumerate(U_PIECES)
         ]
-        w4_early = keep.tile([P, 2 * P * EARLY], U8, name="w4_early", align_bytes=64)
-        w4_late = keep.tile([P, 2 * P * (BANDS - EARLY)], U8, name="w4_late", align_bytes=64)
+        w4_codes = [
+            keep.tile([P, 2 * P * (hi - lo)], U8, name=f"w4_codes{lo}", align_bytes=64) for lo, hi in W4_SPANS
+        ]
         w4_scale_rows = keep.tile([P, M], U8, name="w4_scale_rows", align_bytes=64)
         wgt_rows = keep.tile([P, P], F32, name="wgt_rows")
         b_rows = keep.tile([P, P], F32, name="b_rows")
@@ -72,7 +74,11 @@ def tile_list_hmix_bias_kernel(tc, xT, w4_words, w4_scales, c, u, wgt, b, offs, 
         for i in range(PACK):
             nc.sync.dma_start(planes[i][:], xv[:, i, :])
         nc.sync.dma_start(c_raw[:], cv)
-        nc.sync.dma_start(w4_early[:], w4_words[0, :, 0 : 2 * P * EARLY])
+
+        def load_w4(k):
+            nc.sync.dma_start(w4_codes[k][:], w4_words[0, :, 2 * P * W4_SPANS[k][0] : 2 * P * W4_SPANS[k][1]])
+
+        load_w4(0)
         for q in range(P // QUADRANT):
             nc.sync.dma_start(
                 w4_scale_rows[QUADRANT * q : QUADRANT * q + 4, :].bitcast(I32),
@@ -80,8 +86,8 @@ def tile_list_hmix_bias_kernel(tc, xT, w4_words, w4_scales, c, u, wgt, b, offs, 
             )
         for q, piece in enumerate(U_PIECES):
             nc.sync.dma_start(u_raw[q][:], uv[:, :, P * piece[0] : P * (piece[-1] + 1)])
-            if EARLY + 1 in piece:
-                nc.sync.dma_start(w4_late[:], w4_words[0, :, 2 * P * EARLY : 2 * M])
+            if q >= 2:
+                load_w4(q - 1)
 
         turned = psum.tile([P, P], F32, name="turned", tag="bank6")
         nc.tensor.transpose(turned[:], wgt_rows[:], ident[:])
@@ -147,7 +153,7 @@ def tile_list_hmix_bias_kernel(tc, xT, w4_words, w4_scales, c, u, wgt, b, offs, 
             quantise(c_codes[:, cols], c_scales[:, cols], c_woven[h][:])
 
         def w4_pass(n, cols, acc, start):
-            words, first = (w4_early, 0) if n < EARLY else (w4_late, EARLY)
+            words, first = [(w4_codes[k], lo) for k, (lo, hi) in enumerate(W4_SPANS) if lo <= n < hi][0]
             nc.tensor.matmul_mx(
                 out=acc,
                 lhsT=words[:, 2 * P * (n - first) : 2 * P * (n - first + 1)].bitcast(E2M1X4),

@@ -30,6 +30,7 @@ EARLY = 3
 W4_SPANS = ((0, EARLY), (EARLY, BANDS - 2), (BANDS - 2, BANDS))
 C_SCALAR = 272
 SHARED = BANDS - 2
+STORES = tuple((n,) for n in range(BANDS))
 
 FLOPS = 2 * M * S * (K + L)
 
@@ -89,7 +90,7 @@ def tile_list_hmix_bias_kernel(tc, xT, w4_words, w4_scales, c, u, wgt, b, offs, 
             if q >= 2:
                 load_w4(q - 1)
 
-        turned = psum.tile([P, P], F32, name="turned", tag="bank6")
+        turned = psum.tile([P, P], F32, name="turned", tag="bank4")
         nc.tensor.transpose(turned[:], wgt_rows[:], ident[:])
         nc.vector.tensor_copy(
             wgt_cols[:].rearrange("m q (g r) -> m q g r", g=HEADS),
@@ -183,11 +184,24 @@ def tile_list_hmix_bias_kernel(tc, xT, w4_words, w4_scales, c, u, wgt, b, offs, 
             rows = slice(n * P, (n + 1) * P)
             quantise(u_codes[:, rows], u_scales[:, rows], u_woven[n][:])
 
-        accs = [psum.tile([P, S], F32, name=f"acc{n}", tag=f"bank{n}") for n in range(SHARED)]
+        def banks(n):
+            if n == 0:
+                tags = (0, SHARED)
+            elif n < SHARED:
+                return [(slice(0, S), psum.tile([P, S], F32, name=f"acc{n}", tag=f"bank{n}"))]
+            else:
+                tags = (n, n - SHARED)
+            return [
+                (cols, psum.tile([P, HALF], F32, name=f"acc{n}_{cols.start}", tag=f"bank{bank}"))
+                for cols, bank in zip(HALVES, tags)
+            ]
+
+        accs = {n: banks(n) for n in range(SHARED)}
         for half in HALVES:
             for n in range(EARLY):
+                cols, acc = [part for part in accs[n] if part[0].start <= half.start < part[0].stop][0]
                 for lo in range(half.start, half.stop, P):
-                    w4_pass(n, slice(lo, lo + P), accs[n][:, lo : lo + P], lo == 0)
+                    w4_pass(n, slice(lo, lo + P), acc[:, lo - cols.start : lo - cols.start + P], lo == cols.start)
 
         weave_u(nc.scalar.copy, 0, 0, P)
         weave_u(nc.scalar.copy, 1, 0, P // 2)
@@ -201,23 +215,23 @@ def tile_list_hmix_bias_kernel(tc, xT, w4_words, w4_scales, c, u, wgt, b, offs, 
             quantise_u(n + 1)
 
         reused = {0: "u_raw0", SHARED: f"u_woven{BANDS - 1}"}
-        for n in range(BANDS):
-            bias = b_cols[:, n : n + 1]
-            if n < SHARED:
+        ov = out.rearrange("(n p) s -> p n s", p=P)
+        for piece in STORES:
+            first = piece[0]
+            result = keep.tile(
+                [P, len(piece), S], F32, name=f"result{first}", tag=reused.get(first, f"result{first}"), align_bytes=64
+            )
+            for n in piece:
+                parts = accs[n] if n < SHARED else banks(n)
                 if n >= EARLY:
-                    w4_pass(n, slice(0, S), accs[n][:], True)
-                u_pass(n, slice(0, S), accs[n][:])
-            else:
-                halves = []
-                for cols, bank in zip(HALVES, (n, n - SHARED)):
-                    halves.append(psum.tile([P, HALF], F32, name=f"acc{n}_{cols.start}", tag=f"bank{bank}"))
-                    w4_pass(n, cols, halves[-1][:], True)
-                for cols, acc in zip(HALVES, halves):
+                    for cols, acc in parts:
+                        w4_pass(n, cols, acc[:], True)
+                for cols, acc in parts:
                     u_pass(n, cols, acc[:])
-            result = keep.tile([P, S], F32, name=f"result{n}", tag=reused.get(n, f"result{n}"), align_bytes=64)
-            if n < SHARED:
-                nc.scalar.activation(result[:], accs[n][:], IDENTITY, bias=bias)
-            else:
-                nc.vector.tensor_scalar(result[:, HALVES[0]], halves[0][:], bias, None, ADD)
-                nc.scalar.activation(result[:, HALVES[1]], halves[1][:], IDENTITY, bias=bias)
-            nc.sync.dma_start(out[n * P : (n + 1) * P, :], result[:])
+                bias = b_cols[:, n : n + 1]
+                for cols, acc in parts:
+                    if n >= SHARED and cols.start == 0:
+                        nc.vector.tensor_scalar(result[:, n - first, cols], acc[:], bias, None, ADD)
+                    else:
+                        nc.scalar.activation(result[:, n - first, cols], acc[:], IDENTITY, bias=bias)
+            nc.sync.dma_start(ov[:, first : piece[-1] + 1, :], result[:])

@@ -42,19 +42,19 @@ def tile_list_hmix_bias_kernel(tc, xT, w4_words, w4_scales, c, u, wgt, b, offs, 
         psum = ctx.enter_context(tc.psum_pool(name="psum", bufs=1))
 
         offsets = keep.tile([P, S // GROUP], U16, name="offsets")
-        weights = keep.tile([P, S], F32, name="weights")
-        planes = [keep.tile([P, T], F32, name=f"plane{i}") for i in range(PACK)]
-        c_raw = keep.tile([P, PACK, S], F32, name="c_raw")
+        weights = keep.tile([P, S], F32, name="weights", align_bytes=256)
+        planes = [keep.tile([P, T], F32, name=f"plane{i}", align_bytes=256) for i in range(PACK)]
+        c_raw = keep.tile([P, PACK, S], F32, name="c_raw", align_bytes=256)
         u_raw = [
-            keep.tile([P, PACK, P * len(piece)], F32, name=f"u_raw{q}", tag=f"u_raw{q}", align_bytes=64)
+            keep.tile([P, PACK, P * len(piece)], F32, name=f"u_raw{q}", tag=f"u_raw{q}", align_bytes=256)
             for q, piece in enumerate(U_PIECES)
         ]
         w4_codes = [
-            keep.tile([P, 2 * P * (hi - lo)], U8, name=f"w4_codes{lo}", align_bytes=64) for lo, hi in W4_SPANS
+            keep.tile([P, 2 * P * (hi - lo)], U8, name=f"w4_codes{lo}", align_bytes=256) for lo, hi in W4_SPANS
         ]
-        w4_scale_rows = keep.tile([P, M], U8, name="w4_scale_rows", align_bytes=64)
-        wgt_rows = keep.tile([P, P], F32, name="wgt_rows")
-        b_rows = keep.tile([P, P], F32, name="b_rows")
+        w4_scale_rows = keep.tile([P, M], U8, name="w4_scale_rows", align_bytes=256)
+        wgt_rows = keep.tile([P, P], F32, name="wgt_rows", align_bytes=256)
+        b_rows = keep.tile([P, P], F32, name="b_rows", align_bytes=256)
         wgt_cols = keep.tile([P, RUNS, P], F32, name="wgt_cols")
         ident = keep.tile([P, P], F32, name="ident")
 
@@ -104,20 +104,20 @@ def tile_list_hmix_bias_kernel(tc, xT, w4_words, w4_scales, c, u, wgt, b, offs, 
             nc.tensor.transpose(spread[:, q * P : (q + 1) * P], wgt_cols[:, q, :], ident[:])
         nc.scalar.copy(weights[:], spread[:])
 
-        c_codes = keep.tile([P, S], U32, name="c_codes", align_bytes=64)
-        c_scales = keep.tile([P, S], U8, name="c_scales", align_bytes=64)
+        c_codes = keep.tile([P, S], U32, name="c_codes", align_bytes=256)
+        c_scales = keep.tile([P, S], U8, name="c_scales", align_bytes=256)
         picks_early = keep.tile([P, 2, S], F32, name="picks_early", tag="picks_early")
         picks_late = [keep.tile([P, 2, HALF], F32, name=f"picks_late{h}") for h in range(2)]
         u_woven = [
-            keep.tile([P, P, PACK], BF16, name=f"u_woven{n}", tag=f"u_woven{n}", align_bytes=64) for n in range(BANDS)
+            keep.tile([P, P, PACK], BF16, name=f"u_woven{n}", tag=f"u_woven{n}", align_bytes=256) for n in range(BANDS)
         ]
-        u_codes = keep.tile([P, M], U32, name="u_codes", align_bytes=64)
-        u_scales = keep.tile([P, M], U8, name="u_scales", align_bytes=64)
+        u_codes = keep.tile([P, M], U32, name="u_codes", align_bytes=256)
+        u_scales = keep.tile([P, M], U8, name="u_scales", align_bytes=256)
         xg_woven = [
-            keep.tile([P, HALF, PACK], BF16, name=f"xg_woven{h}", tag=f"xg_woven{h}", align_bytes=64) for h in range(2)
+            keep.tile([P, HALF, PACK], BF16, name=f"xg_woven{h}", tag=f"xg_woven{h}", align_bytes=256) for h in range(2)
         ]
-        xg_codes = keep.tile([P, S], U32, name="xg_codes", align_bytes=64)
-        xg_scales = keep.tile([P, S], U8, name="xg_scales", align_bytes=64)
+        xg_codes = keep.tile([P, S], U32, name="xg_codes", align_bytes=256)
+        xg_scales = keep.tile([P, S], U8, name="xg_scales", align_bytes=256)
 
         def weave(copy, dst, src):
             copy(dst.rearrange("p (r e) i -> p r i e", e=4), src.rearrange("p i (r e) -> p r i e", e=4))
@@ -144,7 +144,7 @@ def tile_list_hmix_bias_kernel(tc, xT, w4_words, w4_scales, c, u, wgt, b, offs, 
             quantise(xg_codes[:, cols], xg_scales[:, cols], xg_woven[h][:])
 
         c_woven = [
-            keep.tile([P, HALF, PACK], BF16, name=f"c_woven{h}", tag=tag, align_bytes=64)
+            keep.tile([P, HALF, PACK], BF16, name=f"c_woven{h}", tag=tag, align_bytes=256)
             for h, tag in enumerate(("c_woven0", "xg_woven1"))
         ]
         weave(nc.scalar.copy, c_woven[0][:], c_raw[:, :, 0:HALF])
@@ -219,7 +219,7 @@ def tile_list_hmix_bias_kernel(tc, xT, w4_words, w4_scales, c, u, wgt, b, offs, 
         for piece in STORES:
             first = piece[0]
             result = keep.tile(
-                [P, len(piece), S], F32, name=f"result{first}", tag=reused.get(first, f"result{first}"), align_bytes=64
+                [P, len(piece), S], F32, name=f"result{first}", tag=reused.get(first, f"result{first}"), align_bytes=256
             )
             for n in piece:
                 parts = accs[n] if n < SHARED else banks(n)

@@ -80,10 +80,10 @@ def tile_list_hmix_bias_kernel(tc, xT, w4_words, w4_scales, c, u, wgt, b, offs, 
             nc.sync.dma_start(w4_codes[k][:], w4_words[0, :, 2 * P * W4_SPANS[k][0] : 2 * P * W4_SPANS[k][1]])
 
         load_w4(0)
-        for q in range(P // QUADRANT):
+        for r in range(PACK):
             nc.sync.dma_start(
-                w4_scale_rows[QUADRANT * q : QUADRANT * q + 4, :].bitcast(I32),
-                w4_scales[0, 4 * q : 4 * q + 4, :].bitcast(I32),
+                w4_scale_rows[r:P:QUADRANT, :].bitcast(I32),
+                w4_scales[0].rearrange("(q r) n -> q r n", r=PACK)[:, r, :].bitcast(I32),
             )
         for q, piece in enumerate(U_PIECES):
             nc.sync.dma_start(u_raw[q][:], uv[:, :, P * piece[0] : P * (piece[-1] + 1)])

from contextlib import ExitStack

import concourse.mybir as mybir
from concourse.masks import make_identity

F32 = mybir.dt.float32
BF16 = mybir.dt.bfloat16
I32 = mybir.dt.int32
U32 = mybir.dt.uint32
U16 = mybir.dt.uint16
U8 = mybir.dt.uint8
E4M3X4 = mybir.dt.float8_e4m3fn_x4
E2M1X4 = mybir.dt.float4_e2m1fn_x4
MULT = mybir.AluOpType.mult
ADD = mybir.AluOpType.add
IDENTITY = mybir.ActivationFunctionType.Identity

P = 128
PACK = 4
QUADRANT = 32
K, L, M, T, S = 512, 512, 1024, 2048, 512
HEADS = 8
GROUP = P // HEADS
RUNS = S // P
BANDS = M // P
HALF = S // 2
HALVES = (slice(0, HALF), slice(HALF, S))
U_PIECES = ((0, 1), (2, 3), (4, 5), (6, 7))
EARLY = 3
W4_SPANS = ((0, EARLY), (EARLY, BANDS - 2), (BANDS - 2, BANDS))
C_SCALAR = 272
SHARED = BANDS - 2
STORES = tuple((n,) for n in range(BANDS))

FLOPS = 2 * M * S * (K + L)


def tile_list_hmix_bias_kernel(tc, xT, w4_words, w4_scales, c, u, wgt, b, offs, out):
    nc = tc.nc
    with ExitStack() as ctx:
        keep = ctx.enter_context(tc.tile_pool(name="keep", bufs=1))
        psum = ctx.enter_context(tc.psum_pool(name="psum", bufs=1))

        offsets = keep.tile([P, S // GROUP], U16, name="offsets")
        weights = keep.tile([P, S], F32, name="weights", align_bytes=256)
        planes = [keep.tile([P, T], F32, name=f"plane{i}", align_bytes=256) for i in range(PACK)]
        c_raw = keep.tile([P, PACK, S], F32, name="c_raw", align_bytes=256)
        u_raw = [
            keep.tile([P, PACK, P * len(piece)], F32, name=f"u_raw{q}", tag=f"u_raw{q}", align_bytes=256)
            for q, piece in enumerate(U_PIECES)
        ]
        w4_codes = [
            keep.tile([P, 2 * P * (hi - lo)], U8, name=f"w4_codes{lo}", align_bytes=256) for lo, hi in W4_SPANS
        ]
        w4_scale_rows = keep.tile([P, M], U8, name="w4_scale_rows", align_bytes=256)
        wgt_rows = keep.tile([P, P], F32, name="wgt_rows", align_bytes=256)
        b_rows = keep.tile([P, P], F32, name="b_rows", align_bytes=256)
        wgt_cols = keep.tile([P, RUNS, P], F32, name="wgt_cols")
        ident = keep.tile([P, P], F32, name="ident")

        xv = xT.rearrange("(p i) t -> p i t", i=PACK)
        cv = c.rearrange("(p i) s -> p i s", i=PACK)
        uv = u.rearrange("(p i) n -> p i n", i=PACK)

        nc.gpsimd.memset(b_rows[:], 0.0)
        nc.gpsimd.memset(w4_scale_rows[:].bitcast(I32), 0)
        nc.vector.memset(wgt_rows[QUADRANT : 2 * QUADRANT, :], 0.0)
        nc.vector.memset(wgt_rows[2 * QUADRANT : P, :], 0.0)
        make_identity(nc, ident[:])

        wgt_runs = wgt.rearrange("(g r) (q m) -> g q r m", r=GROUP, m=P)[:, :, 0, :]
        nc.scalar.dma_start(wgt_rows[0 : HEADS * RUNS, :], wgt_runs)
        nc.scalar.dma_start(b_rows[0:BANDS, :], b.rearrange("(t m) -> t m", m=P))
        nc.sync.dma_start(offsets[:], offs)
        for i in range(PACK):
            nc.sync.dma_start(planes[i][:], xv[:, i, :])
        nc.sync.dma_start(c_raw[:], cv)

        def load_w4(k):
            nc.sync.dma_start(w4_codes[k][:], w4_words[0, :, 2 * P * W4_SPANS[k][0] : 2 * P * W4_SPANS[k][1]])

        load_w4(0)
        for r in range(PACK):
            nc.sync.dma_start(
                w4_scale_rows[r:P:QUADRANT, :].bitcast(I32),
                w4_scales[0].rearrange("(q r) n -> q r n", r=PACK)[:, r, :].bitcast(I32),
            )
        for q, piece in enumerate(U_PIECES):
            nc.sync.dma_start(u_raw[q][:], uv[:, :, P * piece[0] : P * (piece[-1] + 1)])
            if q >= 2:
                load_w4(q - 1)

        turned = psum.tile([P, P], F32, name="turned", tag="bank4")
        nc.tensor.transpose(turned[:], wgt_rows[:], ident[:])
        nc.vector.tensor_copy(
            wgt_cols[:].rearrange("m q (g r) -> m q g r", g=HEADS),
            turned[:, 0 : HEADS * RUNS]
            .rearrange("m (g q) -> m q g", g=HEADS)
            .unsqueeze(3)
            .to_broadcast([P, RUNS, HEADS, GROUP]),
        )
        spread = psum.tile([P, S], F32, name="spread", tag="bank5")
        for q in range(RUNS):
            nc.tensor.transpose(spread[:, q * P : (q + 1) * P], wgt_cols[:, q, :], ident[:])
        nc.scalar.copy(weights[:], spread[:])

        c_codes = keep.tile([P, S], U32, name="c_codes", align_bytes=256)
        c_scales = keep.tile([P, S], U8, name="c_scales", align_bytes=256)
        picks_early = keep.tile([P, 2, S], F32, name="picks_early", tag="picks_early")
        picks_late = [keep.tile([P, 2, HALF], F32, name=f"picks_late{h}") for h in range(2)]
        u_woven = [
            keep.tile([P, P, PACK], BF16, name=f"u_woven{n}", tag=f"u_woven{n}", align_bytes=256) for n in range(BANDS)
        ]
        u_codes = keep.tile([P, M], U32, name="u_codes", align_bytes=256)
        u_scales = keep.tile([P, M], U8, name="u_scales", align_bytes=256)
        xg_woven = [
            keep.tile([P, HALF, PACK], BF16, name=f"xg_woven{h}", tag=f"xg_woven{h}", align_bytes=256) for h in range(2)
        ]
        xg_codes = keep.tile([P, S], U32, name="xg_codes", align_bytes=256)
        xg_scales = keep.tile([P, S], U8, name="xg_scales", align_bytes=256)

        def weave(copy, dst, src):
            copy(dst.rearrange("p (r e) i -> p r i e", e=4), src.rearrange("p i (r e) -> p r i e", e=4))

        def quantise(codes, scales, woven):
            nc.vector.quantize_mx(out=codes.bitcast(E4M3X4), scales=scales, in_=woven.rearrange("p w i -> p (w i)"))

        for i in range(2):
            nc.vector.tensor_tensor(picks_early[:, i, :], planes[i][:].indirect(offsets[:]), weights[:], MULT)
        for h, cols in enumerate(HALVES):
            weave(nc.scalar.copy, xg_woven[h][:, :, 0:2], picks_early[:, :, cols])
        b_cols = keep.tile([P, BANDS], F32, name="b_cols", tag="picks_early")
        b_turned = psum.tile([P, P], F32, name="b_turned", tag="bank7")
        nc.tensor.transpose(b_turned[:], b_rows[:], ident[:])
        nc.scalar.copy(b_cols[:], b_turned[:, 0:BANDS])
        for i in range(2):
            for h, cols in enumerate(HALVES):
                window = planes[2 + i][:].indirect(offsets[:, cols.start // GROUP : cols.stop // GROUP])
                nc.vector.tensor_tensor(picks_late[h][:, i, :], window, weights[:, cols], MULT)
        weave(nc.scalar.copy, xg_woven[0][:, :, 2:4], picks_late[0][:])
        weave(nc.scalar.copy, xg_woven[1][:, 0:P, 2:4], picks_late[1][:, :, 0:P])
        weave(nc.vector.tensor_copy, xg_woven[1][:, P:HALF, 2:4], picks_late[1][:, :, P:HALF])
        for h, cols in enumerate(HALVES):
            quantise(xg_codes[:, cols], xg_scales[:, cols], xg_woven[h][:])

        c_woven = [
            keep.tile([P, HALF, PACK], BF16, name=f"c_woven{h}", tag=tag, align_bytes=256)
            for h, tag in enumerate(("c_woven0", "xg_woven1"))
        ]
        weave(nc.scalar.copy, c_woven[0][:], c_raw[:, :, 0:HALF])
        weave(nc.scalar.copy, c_woven[1][:, 0 : C_SCALAR - HALF, :], c_raw[:, :, HALF:C_SCALAR])
        weave(nc.vector.tensor_copy, c_woven[1][:, C_SCALAR - HALF : HALF, :], c_raw[:, :, C_SCALAR:S])
        for h, cols in enumerate(HALVES):
            quantise(c_codes[:, cols], c_scales[:, cols], c_woven[h][:])

        def w4_pass(n, cols, acc, start):
            words, first = [(w4_codes[k], lo) for k, (lo, hi) in enumerate(W4_SPANS) if lo <= n < hi][0]
            nc.tensor.matmul_mx(
                out=acc,
                lhsT=words[:, 2 * P * (n - first) : 2 * P * (n - first + 1)].bitcast(E2M1X4),
                lhsT_scale=w4_scale_rows[:, P * n : P * (n + 1)],
                rhs=xg_codes[:, cols].bitcast(E4M3X4),
                rhs_scale=xg_scales[:, cols],
                start=start,
                stop=False,
            )

        def u_pass(n, cols, acc):
            nc.tensor.matmul_mx(
                out=acc,
                lhsT=u_codes[:, P * n : P * (n + 1)].bitcast(E4M3X4),
                lhsT_scale=u_scales[:, P * n : P * (n + 1)],
                rhs=c_codes[:, cols].bitcast(E4M3X4),
                rhs_scale=c_scales[:, cols],
                start=False,
                stop=True,
            )

        def weave_u(copy, n, lo, hi):
            q, place = [(q, piece.index(n)) for q, piece in enumerate(U_PIECES) if n in piece][0]
            weave(copy, u_woven[n][:, lo:hi, :], u_raw[q][:, :, place * P + lo : place * P + hi])

        def quantise_u(n):
            rows = slice(n * P, (n + 1) * P)
            quantise(u_codes[:, rows], u_scales[:, rows], u_woven[n][:])

        def banks(n):
            if n == 0:
                tags = (0, SHARED)
            elif n < SHARED:
                return [(slice(0, S), psum.tile([P, S], F32, name=f"acc{n}", tag=f"bank{n}"))]
            else:
                tags = (n, n - SHARED)
            return [
                (cols, psum.tile([P, HALF], F32, name=f"acc{n}_{cols.start}", tag=f"bank{bank}"))
                for cols, bank in zip(HALVES, tags)
            ]

        accs = {n: banks(n) for n in range(SHARED)}
        for half in HALVES:
            for n in range(EARLY):
                cols, acc = [part for part in accs[n] if part[0].start <= half.start < part[0].stop][0]
                for lo in range(half.start, half.stop, P):
                    w4_pass(n, slice(lo, lo + P), acc[:, lo - cols.start : lo - cols.start + P], lo == cols.start)

        weave_u(nc.scalar.copy, 0, 0, P)
        weave_u(nc.scalar.copy, 1, 0, P // 2)
        weave_u(nc.vector.tensor_copy, 1, P // 2, P)
        quantise_u(0)
        quantise_u(1)
        for n in range(2, BANDS, 2):
            weave_u(nc.vector.tensor_copy, n, 0, P)
            weave_u(nc.vector.tensor_copy, n + 1, 0, P)
            quantise_u(n)
            quantise_u(n + 1)

        reused = {0: "u_raw0", SHARED: f"u_woven{BANDS - 1}"}
        ov = out.rearrange("(n p) s -> p n s", p=P)
        for piece in STORES:
            first = piece[0]
            result = keep.tile(
                [P, len(piece), S], F32, name=f"result{first}", tag=reused.get(first, f"result{first}"), align_bytes=256
            )
            for n in piece:
                parts = accs[n] if n < SHARED else banks(n)
                if n >= EARLY:
                    for cols, acc in parts:
                        w4_pass(n, cols, acc[:], True)
                for cols, acc in parts:
                    u_pass(n, cols, acc[:])
                bias = b_cols[:, n : n + 1]
                for cols, acc in parts:
                    if n >= SHARED and cols.start == 0:
                        nc.vector.tensor_scalar(result[:, n - first, cols], acc[:], bias, None, ADD)
                    else:
                        nc.scalar.activation(result[:, n - first, cols], acc[:], IDENTITY, bias=bias)
            nc.sync.dma_start(ov[:, first : piece[-1] + 1, :], result[:])
